import numpy as np, ml_dtypes
CORES = [2,3,42,43,82,83,122,123]
N = 8
import mx_ref
BF = ml_dtypes.bfloat16
def cols(t, e):
    v = np.concatenate([t.reshape(128, -1, 4), np.zeros((128, 1, 4), BF)], axis=1)
    return np.ascontiguousarray(v[:, e]).reshape(128, -1)
def f(rng, *shape):
    return mx_ref.flush((rng.standard_normal(shape, dtype=np.float32) * np.exp2(rng.integers(-2, 3, shape[:-1] + (1,)))).astype(BF))
def wide(rng, *shape, cols=0):
    v = rng.standard_normal(shape, dtype=np.float32) * np.exp2(rng.integers(-12, 13, shape)).astype(np.float32)
    if cols: v *= np.repeat(np.exp2(rng.integers(-cols, cols + 1, shape[:-2] + (1, shape[-1] // 4))) * (rng.random(shape[:-2] + (1, shape[-1] // 4)) > 0.0625), 4, axis=-1).astype(np.float32)
    return mx_ref.flush(v.astype(BF))
T, G, C = 256, 8, 16
def lean(rng, d, sizes):
    p, t = rng.integers(0, 128), rng.integers(0, 4)
    q, v = np.array(d["qw"]), np.array(d["x"])
    q[:, p, t::4] = BF(128)
    v[:, p, t::4] = np.repeat(np.asarray(sizes, np.float32), 16).astype(BF)
    return {"qw": q, "x": v}
def setup_inputs(rng):
    return {"qw": f(rng, N, 128, 512), "x": f(rng, N, 128, 4 * T)}
def setup_inputs_ties(rng):
    d = setup_inputs(rng); v = []
    for s in range(N):
        k = rng.permutation(np.arange(C) // 4)
        v.append(cols(d["x"][s], np.concatenate([16 * c + rng.permutation(16) for c in k])))
    d["x"] = np.stack(v); return d
def setup_inputs_last(rng):
    return lean(rng, setup_inputs(rng), [0] * (C - 1) + [128])
def setup_inputs_alike(rng):
    d = setup_inputs(rng); d["qw"] = np.concatenate([d["qw"][:, :, :64]] * G, axis=2); return d
def setup_inputs_below(rng):
    return lean(rng, setup_inputs(rng), [-128 * 4096] * C)
def setup_inputs_spread(rng):
    d = setup_inputs(rng); d["x"] = wide(rng, N, 128, 4 * T); return d
def check_inputs(d):
    b = []
    for k in ("qw", "x"):
        a = np.abs(np.asarray(d[k]).astype(np.float32))
        if not ((a == 0) | ((a >= 2.0 ** -30) & (a <= 2.0 ** 30))).all(): b.append(k)
    return b
def decode(q, n):
    out = np.zeros((128, 4 * n), np.float32)
    for b in range(4):
        e = np.zeros((128, 128, 4), np.float32); e[np.arange(128), np.arange(128), b] = 1
        out[:, b::4] = mx_ref.matmul(mx_ref.quantize(e.reshape(128, 512).astype(BF)), q)
    return out
def reference(qw, x):
    W = [mx_ref.quantize(qw[r]) for r in range(N)]
    X = [mx_ref.quantize(x[s]) for s in range(N)]
    R = [mx_ref.quantize((x[s].astype(np.float32) - decode(X[s], T)).astype(BF)) for s in range(N)]
    y = np.zeros((N, 128, N * G * 16), np.float32); ch = np.zeros((N, G, N), np.float32)
    for r in range(N):
        for s in range(N):
            a, b = mx_ref.matmul(W[r], X[s]), mx_ref.matmul(W[r], R[s])
            best = a.reshape(G, 16, C, 16).max(axis=(1, 3)).argmax(axis=1)
            ch[r][:, s] = best
            for g in range(G):
                i, j = 16 * (s * G + g), 16 * int(best[g])
                y[r][:, i:i + 16] = a[:, j:j + 16] + b[:, j:j + 16]
    return {"y": y, "ch": ch}

@@ -1,0 +1,440 @@
+from concourse.bass import DstId, RemoteDMATransfer
+from concourse.mybir import dt, AluOpType, ActivationFunctionType, AxisListType
+
+NR, Q, IT = 8, 128, 256
+LOW = -5.0e29
+NB = 3
+NI = 5
+
+SCRATCH = {
+    "qt": ("sbuf", [128, 4 * Q], "bfloat16"),
+    "xr": ("sbuf", [128, 8 * IT], "bfloat16"),
+    "onb": ("sbuf", [128, 516], "bfloat16"),
+    "onf": ("sbuf", [128, 128], "float32"),
+    "zt": ("sbuf", [128, 516], "bfloat16"),
+    "ident": ("sbuf", [128, 128], "float32"),
+    "pm": ("sbuf", [128, 128], "float32"),
+    "rst": ("sbuf", [128, 256], "float32"),
+    "neg": ("sbuf", [128, 256], "float32"),
+    "eq": ("sbuf", [128, 512], "float8_e4m3fn_x4"),
+    "es": ("sbuf", [128, 512], "uint8"),
+    "wq": ("sbuf", [128, NR * Q], "float8_e4m3fn_x4"),
+    "ws": ("sbuf", [128, NR * Q], "uint8"),
+    "xq": ("sbuf", [128, 2 * IT], "float8_e4m3fn_x4"),
+    "xs": ("sbuf", [128, 2 * IT], "uint8"),
+    "pq": ("sbuf", [128, 2 * IT], "float8_e4m3fn_x4"),
+    "ps": ("sbuf", [128, 2 * IT], "uint8"),
+    "fq": ("sbuf", [128, 2 * IT], "float8_e4m3fn_x4"),
+    "fs": ("sbuf", [128, 2 * IT], "uint8"),
+    "S": ("sbuf", [128, 2304], "float32"),
+    "P": ("sbuf", [128, 1024], "float32"),
+    "lt": ("sbuf", [128, 64], "float32"),
+    "cc": ("sbuf", [128, 16], "float32"),
+    "bc": ("sbuf", [128, 512], "float32"),
+    "of": ("sbuf", [128, 256], "uint16"),
+    "gt": ("sbuf", [128, NI * 1024], "bfloat16"),
+    "cq": ("sbuf", [128, NI * 256], "float8_e4m3fn_x4"),
+    "cs": ("sbuf", [128, NI * 256], "uint8"),
+    "lq": ("sbuf", [128, NR * 256], "float8_e4m3fn_x4"),
+    "ls": ("sbuf", [128, NR * 256], "uint8"),
+    "ab": ("sbuf", [128, 3 * IT], "float32"),
+    "yt": ("sbuf", [128, 1024], "float32"),
+    "cht": ("sbuf", [32, 32], "float32"),
+    "chu": ("sbuf", [32, 32], "float32"),
+    "cho": ("sbuf", [32, 8], "float32"),
+    "nx": ("sbuf", [128, 1], "float32"),
+    "nb": ("dram", [1, 128, 1], "float32"),
+    "nl": ("dram", [NR, 128, 1], "float32"),
+    "sc0": ("psum", [128, 512], "float32"),
+    "sc1": ("psum", [128, 512], "float32"),
+    "tr": ("psum", [128, 512], "float32"),
+    "ob": ("psum", [128, 512], "float32"),
+    "y0": ("psum", [128, 512], "float32"),
+    "y1": ("psum", [128, 512], "float32"),
+    "y2": ("psum", [128, 512], "float32"),
+    "y3": ("psum", [128, 512], "float32"),
+}
+SEMAPHORES = (
+    ["ldq", "ldx", "kone", "ms", "mz", "kz", "kid", "kpm", "eqd", "wqd", "xqd", "rs", "rq", "lsem", "pa", "pf", "nm", "nx",
+     "nz", "nd", "ct", "sc", "sy", "fa0", "fa1", "fa2", "fb", "fg", "ch1", "ch2", "ch3"]
+    + ["dm%d" % b for b in range(4)]
+    + ["%s%d" % (k, b) for b in range(4) for k in ("mma", "mmb", "saa", "sab", "trd", "s2", "ltd", "cb", "bcd", "obd", "ofd")]
+    + ["%s%d" % (k, i) for i in range(NI) for k in ("gx", "gr", "qz", "fm", "fy")]
+    + ["w%d" % r for r in range(NR)] + ["c%d" % r for r in range(NR)] + ["hc%d" % i for i in range(NI)]
+)
+
+
+def rank_program(g, core, T, topo):
+    cores = list(T.cores)
+    groups, chips = [], []
+    for r in range(len(cores)):
+        c = topo.chip(cores[r])
+        if c not in chips:
+            chips.append(c)
+            groups.append([])
+        groups[chips.index(c)].append(r)
+    ng = len(groups)
+    place = {}
+    for k in range(ng):
+        for j in range(len(groups[k])):
+            place[groups[k][j]] = (k, j)
+    step = sorted(range(1, ng), key=lambda d: topo.same_plane(chips[0], chips[d]))
+
+    def same(r, s):
+        return place[r][1] == place[s][1]
+
+    def peer_of(r):
+        k, j = place[r]
+        return groups[(k + step[-1]) % ng][j]
+
+    def sources(r, b):
+        return sorted([s for s in groups[(place[r][0] - step[b]) % ng] if s != peer_of(r)], key=lambda s: same(r, s))
+
+    def owners(r, b):
+        return [s for s in groups[(place[r][0] + step[b]) % ng] if s != peer_of(r)]
+
+    def relayed(b, r, s):
+        return b < NB - 1 and not same(r, s)
+
+    def helper_of(r):
+        own = cores[r]
+        far = [c for c in topo.cores_of(own) if topo.die(c) != topo.die(own) and T.rank_of(c) is None
+               and all(topo.may_write(c, t) for t in cores)]
+        return far[place[r][1]]
+
+    queue = {"g": g, "v": g.vector, "s": g.scalar, "t": g.tensor, "y": g.sync}
+    cnt, seen, top = {}, {}, {}
+
+    def inc(ins, name, k=1):
+        ins.then_inc(T.sem[name], k)
+        cnt[name] = cnt.get(name, 0) + k
+
+    def wait(q, name):
+        v = cnt[name]
+        if seen.get((q, name), 0) < v:
+            queue[q].wait_ge(T.sem[name], v)
+            seen[(q, name)] = v
+            top[name] = max(top.get(name, 0), v)
+
+    def expect(name, k):
+        cnt[name] = cnt.get(name, 0) + k
+
+    def finish():
+        for name in cnt:
+            if top.get(name, 0) < cnt[name]:
+                wait("g", name)
+
+    far_core = [c for c in cores if topo.chip(c) != topo.chip(core)][0]
+    offe = topo.engines(core, far_core)
+
+    def mask_to(dst):
+        if topo.chip(dst) != topo.chip(core):
+            return topo.mask(core, dst)
+        return sum(1 << e for e in topo.engines(core, dst) if e not in offe)
+
+    def send(dsts, src, dst, sem, mask=None):
+        m = mask_to(dsts[0]) if mask is None else mask
+        if len(dsts) == 1:
+            rid, pid, _ = topo.addr(dsts[0])
+            g.remote_dma(out_ap=dst, in_ap=src, remote_sem=T.sem[sem], local_sem=T.sem["lsem"], pid=pid,
+                         routing_id=rid, dma_engine_mask=m)
+        else:
+            ids = []
+            for d in dsts:
+                rid, pid, _ = topo.addr(d)
+                ids.append(DstId(rid=rid, pnc=pid))
+            g.remote_dma_fused([RemoteDMATransfer(dst_ids=ids, dma_engine_mask=m, remote_sem=T.sem[sem], srcs=[src],
+                                                  dsts=[dst] * len(dsts))], local_sem=T.sem["lsem"])
+        cnt["lsem"] = cnt.get("lsem", 0) + bin(m).count("1")
+
+    n_off, n_on = len(offe), len([e for e in topo.engines(core, [c for c in topo.cores_of(core) if c != core][0])
+                                  if e not in offe])
+
+    def send_xr(dst, codes, plane, codes2, plane2, sem):
+        send([dst], codes[:, :].bitcast(dt.uint8), codes2[:, :].bitcast(dt.uint8), sem)
+        send([dst], plane[:, :], plane2[:, :], sem)
+
+    def send_c(dst, i, s):
+        send([dst], T.cq[:, 256 * i:256 * i + 256].bitcast(dt.uint8), T.lq[:, 256 * s:256 * s + 256].bitcast(dt.uint8), "c%d" % s)
+        send([dst], T.cs[:, 256 * i:256 * i + 256], T.ls[:, 256 * s:256 * s + 256], "c%d" % s)
+
+    rank = T.rank_of(core)
+    if rank is None:
+        for r in range(len(cores)):
+            if helper_of(r) == core:
+                expect("pa", 2 * n_on)
+                wait("g", "pa")
+                send_xr(cores[peer_of(r)], T.pq, T.ps, T.fq, T.fs, "pf")
+                for b in range(NB):
+                    for j, d in enumerate(sources(r, b)):
+                        if relayed(b, d, r):
+                            i = 2 * b + j
+                            expect("hc%d" % i, 2 * n_on)
+                            wait("g", "hc%d" % i)
+                            send_c(cores[d], i, r)
+                finish()
+        return
+
+    m, _ = place[rank]
+    duo = groups[m]
+    mate = [r for r in duo if r != rank][0]
+    peer = peer_of(rank)
+    near = duo + [peer]
+    helper = helper_of(rank)
+    v, pe, act, sy = g.vector, g.tensor, g.scalar, g.sync
+    COPY = ActivationFunctionType.Copy
+    ADD, MAX = AluOpType.add, AluOpType.max
+
+    inc(sy.dma_start(T.qt[:, :], T.qw[:, :]), "ldq", 16)
+    inc(sy.dma_start(T.xr[:, 0:4 * IT], T.x[:, :]), "ldx", 16)
+
+    inc(v.memset(T.onb[:, :], 1.0), "kone")
+    inc(v.memset(T.onf[:, :], 1.0), "kone")
+    inc(v.memset(T.rst[:, :], 0.0), "mz")
+    inc(v.memset(T.bc[:, :], 0.0), "ms")
+    inc(v.memset(T.neg[:, :], LOW), "ms")
+    inc(v.memset(T.cht[:, :], 0.0), "ms")
+    inc(v.memset(T.cc[:, :], 0.0), "ms")
+    wait("v", "mz")
+    inc(v.memset(T.rst[:, 0:256:16], LOW), "ms")
+    wait("g", "kone")
+    inc(g.affine_select(T.zt[:, :], T.onb[:, :], [[-1, 516]], AluOpType.is_equal, 0.0, 3, 4), "kz")
+    inc(g.affine_select(T.ident[:, :], T.onf[:, :], [[-1, 128]], AluOpType.is_equal, 0.0, 0, 1), "kid")
+
+    wait("v", "ldq")
+    w0 = Q * rank
+    wcols = T.wq[:, w0:w0 + Q], T.ws[:, w0:w0 + Q]
+    inc(v.quantize_mx(wcols[0], wcols[1], T.qt[:, :]), "wqd")
+    wait("g", "wqd")
+    for b in range(NB):
+        to = [cores[s] for s in owners(rank, b)]
+        send(to, wcols[0].bitcast(dt.uint8), wcols[0].bitcast(dt.uint8), "w%d" % rank)
+        send(to, wcols[1], wcols[1], "w%d" % rank)
+
+    wait("v", "ldx")
+    inc(v.quantize_mx(T.xq[:, 0:IT], T.xs[:, 0:IT], T.xr[:, 0:4 * IT]), "xqd")
+    wait("v", "kz")
+    for b in range(4):
+        inc(v.quantize_mx(T.eq[:, 128 * b:128 * b + 128], T.es[:, 128 * b:128 * b + 128], T.zt[:, 3 - b:3 - b + 512]), "eqd")
+    wait("t", "xqd")
+    wait("t", "eqd")
+    ybank = [T.y0, T.y1, T.y2, T.y3]
+    for b in range(4):
+        inc(pe.matmul_mx(ybank[b][:, 0:IT], T.eq[:, 128 * b:128 * b + 128], T.es[:, 128 * b:128 * b + 128],
+                         T.xq[:, 0:IT], T.xs[:, 0:IT], True, True), "dm%d" % b)
+    for b in range(4):
+        wait("v", "dm%d" % b)
+        inc(v.tensor_tensor(T.xr[:, 4 * IT + b:8 * IT:4], T.xr[:, b:4 * IT:4], ybank[b][:, 0:IT], AluOpType.subtract), "rs")
+    wait("v", "rs")
+    inc(v.quantize_mx(T.xq[:, IT:2 * IT], T.xs[:, IT:2 * IT], T.xr[:, 4 * IT:8 * IT]), "rq")
+    wait("g", "rq")
+    for to in (helper, cores[mate]):
+        send_xr(to, T.xq, T.xs, T.pq, T.ps, "pa")
+    inc(g.iota(T.pm[:, :], [[0, 8], [1, 16]], 0, 0, allow_small_or_imprecise_dtypes=True), "kpm")
+
+    wait("y", "ms")
+    inc(sy.dma_start(T.nb[0:1, :, 0], T.bc[64:65, 0:128]), "nz", 16)
+    wait("y", "nz")
+
+    own = {rank: (T.xq, T.xs), mate: (T.pq, T.ps), peer: (T.fq, T.fs)}
+    banks = {rank: (T.sc0, T.sc1), mate: (T.y0, T.y1), peer: (T.y2, T.y3)}
+
+    def width(b):
+        return len(near) if b == NB else len(sources(rank, b))
+
+    def products(b):
+        if b < NB:
+            src = sources(rank, b)
+            for r in src:
+                expect("w%d" % r, 2 * n_off)
+                wait("t", "w%d" % r)
+            c0, n = Q * min(src), Q * len(src)
+            for h in range(2):
+                if b:
+                    wait("t", ("saa%d", "sab%d")[h] % (b - 1))
+                inc(pe.matmul_mx(banks[rank][h][:, 0:n], T.xq[:, 128 * h:128 * h + 128], T.xs[:, 128 * h:128 * h + 128],
+                                 T.wq[:, c0:c0 + n], T.ws[:, c0:c0 + n], True, True), ("mma%d", "mmb%d")[h] % b)
+            return
+        expect("pa", 2 * n_on)
+        expect("pf", 2 * n_off)
+        for f in ("rs", "wqd", "rq", "saa%d" % (b - 1), "sab%d" % (b - 1)):
+            wait("t", f)
+        for s in (rank, mate, peer):
+            if s != rank:
+                wait("t", "pa" if s == mate else "pf")
+            for h in range(2):
+                inc(pe.matmul_mx(banks[s][h][:, 0:128], own[s][0][:, 128 * h:128 * h + 128], own[s][1][:, 128 * h:128 * h + 128],
+                                 wcols[0], wcols[1], True, True), ("mma%d", "mmb%d")[h] % b)
+
+    def over_queries(b):
+        o, n = 512 * b, 128 * width(b)
+        wait("v", "ms")
+        for h in range(2):
+            wait("v", ("mma%d", "mmb%d")[h] % b)
+            parts = [(n, banks[rank][h], 0)] if b < NB else [(128, banks[s][h], 128 * l) for l, s in enumerate(near)]
+            for w, bank, at in parts:
+                q = o + n * h + at
+                inc(v.tensor_tensor_scan(T.S[:, q:q + w], T.rst[:, 0:w], bank[:, 0:w], 0.0, ADD, MAX), ("saa%d", "sab%d")[h] % b)
+        wait("t", "kid")
+        if b:
+            wait("t", "s2%d" % (b - 1))
+        for h in range(2):
+            wait("t", ("saa%d", "sab%d")[h] % b)
+            inc(pe.transpose(T.tr[0:n // 16, 128 * h:128 * h + 128], T.S[:, o + n * h + 15:o + n * h + n:16], T.ident[:, :]), "trd%d" % b)
+
+    def over_items(b):
+        p, k = 256 * b, 8 * width(b)
+        wait("v", "trd%d" % b)
+        inc(v.tensor_tensor_scan(T.P[0:k, p:p + 256], T.tr[0:k, 0:256], T.neg[0:k, :], LOW, MAX, MAX), "s2%d" % b)
+        wait("v", "s2%d" % b)
+        inc(v.tensor_scalar(T.lt[0:k, 16 * b:16 * b + 16], T.P[0:k, p + 15:p + 256:16], T.P[0:k, p + 255:p + 256], 64.0,
+                            AluOpType.is_lt, AluOpType.mult), "ltd%d" % b)
+        wait("v", "ltd%d" % b)
+        col = T.cc[0:k, 4 * b:4 * b + 1]
+        inc(v.tensor_reduce(col, T.lt[0:k, 16 * b:16 * b + 16], AxisListType.X, ADD), "cb%d" % b)
+        wait("v", "cb%d" % b)
+        wait("v", "kpm")
+        if b < NB:
+            inc(v.tensor_scalar(T.bc[0:k, 128 * b:128 * b + 128], T.pm[0:k, :], col, None, ADD), "bcd%d" % b)
+            if b < NB - 1:
+                wait("y", "cb%d" % b)
+                q = 8 * min(sources(rank, b))
+                inc(sy.dma_start(T.nb[0:1, q:q + k, 0], col), "nd", 16)
+        else:
+            inc(v.tensor_scalar(T.bc[0:k, 128 * b:128 * b + 128], T.pm[0:k, :], 4.0, col, AluOpType.mult, ADD), "bcd%d" % b)
+        wait("t", "bcd%d" % b)
+        if b:
+            wait("t", "ofd%d" % (b - 1))
+        inc(pe.transpose(T.ob[:, 0:128], T.bc[:, 128 * b:128 * b + 128], T.ident[:, :]), "obd%d" % b)
+
+    def offsets(b):
+        k = 8 * width(b)
+        wait("v", "obd%d" % b)
+        if b < NB:
+            for u in range(4):
+                inc(v.tensor_scalar(T.of[:, 64 * b + u:64 * b + 4 * k:4], T.ob[:, 0:k], float(16 * u), None, ADD), "ofd%d" % b)
+        else:
+            inc(v.tensor_scalar(T.of[:, 64 * b:64 * b + k], T.ob[:, 0:k], 0.25, None, AluOpType.mult), "ofd%d" % b)
+        wait("v", "ofd%d" % b)
+
+    def lists(b, j):
+        src = sources(rank, b)
+        return 64 * b + 32 * sorted(src).index(src[j])
+
+    def gather_x(b, j, q, a, e):
+        i, f = 2 * b + j, lists(b, j)
+        out, win = T.gt[:, 1024 * i + a:1024 * i + e], T.xr[:, 0:1024].indirect(T.of[:, f + a // 16:f + e // 16])
+        wait(q, "ofd%d" % b)
+        inc(v.tensor_copy(out, win) if q == "v" else act.activation(out, win, COPY), "gx%d" % i if q == "v" else "gr%d" % i)
+
+    def gather_r(b, j):
+        i, f = 2 * b + j, lists(b, j)
+        wait("s", "ofd%d" % b)
+        wait("s", "rs")
+        inc(act.activation(T.gt[:, 1024 * i + 512:1024 * i + 1024], T.xr[:, 1024:2048].indirect(T.of[:, f:f + 32]), COPY), "gr%d" % i)
+
+    def pack(b, j):
+        i = 2 * b + j
+        wait("v", "gx%d" % i)
+        wait("v", "gr%d" % i)
+        inc(v.quantize_mx(T.cq[:, 256 * i:256 * i + 256], T.cs[:, 256 * i:256 * i + 256], T.gt[:, 1024 * i:1024 * i + 1024]), "qz%d" % i)
+
+    def ship(b, j):
+        i, d = 2 * b + j, sources(rank, b)[j]
+        wait("g", "qz%d" % i)
+        if relayed(b, d, rank):
+            send([helper], T.cq[:, 256 * i:256 * i + 256].bitcast(dt.uint8), T.cq[:, 256 * i:256 * i + 256].bitcast(dt.uint8), "hc%d" % i)
+            send([helper], T.cs[:, 256 * i:256 * i + 256], T.cs[:, 256 * i:256 * i + 256], "hc%d" % i)
+        else:
+            send_c(cores[d], i, rank)
+
+    products(0)
+    over_queries(0)
+    over_items(0)
+    offsets(0)
+    for b in range(NB):
+        last = b == NB - 1
+        items = range(width(b))
+        for j in items:
+            gather_r(b, j)
+        if not last:
+            gather_x(b, 1, "s", 256, 512)
+        gather_x(b, 0, "v", 0, 512)
+        if not last:
+            products(b + 1)
+            over_queries(b + 1)
+        pack(b, 0)
+        if not last:
+            gather_x(b, 1, "v", 0, 256)
+            pack(b, 1)
+            over_items(b + 1)
+            offsets(b + 1)
+        for j in items:
+            ship(b, j)
+        if b == NB - 2:
+            wait("g", "nd")
+            send([cores[o] for k in range(NB - 1) for o in sources(rank, k)], T.nb[0], T.nl[rank], "nm", 1 << offe[-1])
+            wait("g", "cb%d" % (NB - 1))
+            send([cores[sources(rank, NB - 1)[0]]], T.cc[:, 4 * NB - 4:4 * NB - 3], T.nx[:, :], "nx")
+
+    order = [(T.y1, "sab%d" % NB), (T.y2, "saa%d" % NB), (T.y3, "sab%d" % NB), (T.y0, "fb")]
+    tiles = [(b, s) for b in range(NB) for s in owners(rank, b)]
+    tiles.sort(key=lambda e: (2 + 2 * e[0]) if relayed(e[0], e[1], rank) else (0, 1, 3)[e[0]])
+
+    def final(l):
+        for p in l:
+            s = tiles[p][1]
+            bank = order[p % 4][0]
+            expect("c%d" % s, 2 * n_off)
+            wait("t", order[p][1] if p < 4 else "fy%d" % (p - 4))
+            wait("t", "c%d" % s)
+            pe.matmul_mx(bank[:, 0:128], wcols[0], wcols[1], T.lq[:, 256 * s:256 * s + 128], T.ls[:, 256 * s:256 * s + 128], True, False)
+            inc(pe.matmul_mx(bank[:, 0:128], wcols[0], wcols[1], T.lq[:, 256 * s + 128:256 * s + 256],
+                             T.ls[:, 256 * s + 128:256 * s + 256], False, True), "fm%d" % p)
+            wait("s", "fm%d" % p)
+            inc(act.activation(T.yt[:, 128 * s:128 * s + 128], bank[:, 0:128], COPY), "fy%d" % p)
+            wait("s", "fy%d" % p)
+            inc(act.dma_start(T.y[:, 128 * s:128 * s + 128], T.yt[:, 128 * s:128 * s + 128]), "sy", 16)
+
+    b = NB
+    products(b)
+    over_queries(b)
+    wide = (T.sc0, T.sc1, T.y0)
+    for l, s in enumerate(near):
+        wait("t", ("saa%d" if l != 1 else "sab%d") % b)
+        pe.matmul_mx(wide[l][:, 0:IT], wcols[0], wcols[1], own[s][0][:, 0:IT], own[s][1][:, 0:IT], True, False)
+        inc(pe.matmul_mx(wide[l][:, 0:IT], wcols[0], wcols[1], own[s][0][:, IT:2 * IT], own[s][1][:, IT:2 * IT], False, True), "fa%d" % l)
+        wait("s", "fa%d" % l)
+        inc(act.activation(T.ab[:, IT * l:IT * l + IT], wide[l][:, 0:IT], COPY), "fb")
+    final(range(0, 2))
+    over_items(b)
+    wait("y", "cb%d" % b)
+    inc(sy.dma_start(T.cht[duo[0]:duo[0] + 2, 0:8], T.cc[0:16, 4 * b:4 * b + 1]), "ct", 16)
+    inc(sy.dma_start(T.cht[peer:peer + 1, 0:8], T.cc[16:24, 4 * b:4 * b + 1]), "ct", 16)
+    offsets(b)
+    wait("v", "fb")
+    for l, s in enumerate(near):
+        f0 = 64 * b + 8 * l
+        inc(v.tensor_copy(T.yt[:, 128 * s:128 * s + 128], T.ab[:, IT * l:IT * l + IT].indirect(T.of[:, f0:f0 + 8])), "fg")
+    wait("s", "fg")
+    inc(act.dma_start(T.y[:, 128 * duo[0]:128 * duo[0] + 256], T.yt[:, 128 * duo[0]:128 * duo[0] + 256]), "sy", 16)
+    inc(act.dma_start(T.y[:, 128 * peer:128 * peer + 128], T.yt[:, 128 * peer:128 * peer + 128]), "sy", 16)
+    final(range(2, NI))
+
+    expect("nm", sum(len(owners(rank, k)) for k in range(NB - 1)))
+    expect("nx", n_off)
+    wait("y", "nm")
+    for k in range(NB - 1):
+        s = owners(rank, k)[0]
+        inc(sy.dma_start(T.cht[s:s + 2, 0:8], T.nl[s:s + 2, 8 * rank:8 * rank + 8, 0]), "ct", 16)
+    wait("v", "ct")
+    inc(v.transpose(T.chu[:, :], T.cht[:, :]), "ch1")
+    wait("v", "ch1")
+    inc(v.tensor_scalar(T.cho[0:8, 0:8], T.chu[0:8, 0:8], 1.0 / 64.0, None, AluOpType.mult), "ch2")
+    wait("v", "ch2")
+    wait("v", "nx")
+    s = owners(rank, NB - 1)[0]
+    inc(v.tensor_scalar(T.cho[0:8, s:s + 1], T.nx[0:8, :], 1.0 / 64.0, None, AluOpType.mult), "ch3")
+    wait("y", "ch3")
+    inc(sy.dma_start(T.ch[:, :], T.cho[0:8, 0:8]), "sc", 16)
+    finish()

@@ -3,8 +3,13 @@ from concourse.mybir import dt, AluOpType, ActivationFunctionType, AxisListType
 
 NR, Q, IT = 8, 128, 256
 LOW = -5.0e29
-NB = 3
-NI = 5
+NCORES = 128
+OPT = {
+    "route": {("x", 0): "cr", ("R", 0): "c", ("x", 1): "b", ("R", 1): "b"},
+    "split": True,
+    "vx": 384,
+    "order": ["t1", "fwd", "num", "t2", "t3", "near0", "near1", "fin1", "pick", "fin3", "fin2", "ab0", "ab1", "rows", "last"],
+}
 
 SCRATCH = {
     "qt": ("sbuf", [128, 4 * Q], "bfloat16"),
@@ -14,37 +19,32 @@ SCRATCH = {
     "zt": ("sbuf", [128, 516], "bfloat16"),
     "ident": ("sbuf", [128, 128], "float32"),
     "pm": ("sbuf", [128, 128], "float32"),
+    "unit": ("sbuf", [128, 1], "float32"),
     "rst": ("sbuf", [128, 256], "float32"),
     "neg": ("sbuf", [128, 256], "float32"),
     "eq": ("sbuf", [128, 512], "float8_e4m3fn_x4"),
     "es": ("sbuf", [128, 512], "uint8"),
-    "wq": ("sbuf", [128, NR * Q], "float8_e4m3fn_x4"),
-    "ws": ("sbuf", [128, NR * Q], "uint8"),
+    "wq": ("sbuf", [128, 3 * Q], "float8_e4m3fn_x4"),
+    "ws": ("sbuf", [128, 3 * Q], "uint8"),
     "xq": ("sbuf", [128, 2 * IT], "float8_e4m3fn_x4"),
     "xs": ("sbuf", [128, 2 * IT], "uint8"),
-    "pq": ("sbuf", [128, 2 * IT], "float8_e4m3fn_x4"),
-    "ps": ("sbuf", [128, 2 * IT], "uint8"),
-    "fq": ("sbuf", [128, 2 * IT], "float8_e4m3fn_x4"),
-    "fs": ("sbuf", [128, 2 * IT], "uint8"),
-    "S": ("sbuf", [128, 2304], "float32"),
-    "P": ("sbuf", [128, 1024], "float32"),
-    "lt": ("sbuf", [128, 64], "float32"),
-    "cc": ("sbuf", [128, 16], "float32"),
-    "bc": ("sbuf", [128, 512], "float32"),
-    "of": ("sbuf", [128, 256], "uint16"),
-    "gt": ("sbuf", [128, NI * 1024], "bfloat16"),
-    "cq": ("sbuf", [128, NI * 256], "float8_e4m3fn_x4"),
-    "cs": ("sbuf", [128, NI * 256], "uint8"),
-    "lq": ("sbuf", [128, NR * 256], "float8_e4m3fn_x4"),
-    "ls": ("sbuf", [128, NR * 256], "uint8"),
-    "ab": ("sbuf", [128, 3 * IT], "float32"),
+    "aq": ("sbuf", [128, 8 * IT], "float8_e4m3fn_x4"),
+    "as": ("sbuf", [128, 8 * IT], "uint8"),
+    "S": ("sbuf", [128, 1536], "float32"),
+    "P": ("sbuf", [128, 512], "float32"),
+    "lt": ("sbuf", [128, 32], "float32"),
+    "cc": ("sbuf", [128, 8], "float32"),
+    "bc": ("sbuf", [128, 384], "float32"),
+    "of": ("sbuf", [128, 192], "uint16"),
+    "gt": ("sbuf", [128, 3 * 1024], "bfloat16"),
+    "cq": ("sbuf", [128, 3 * 256], "float8_e4m3fn_x4"),
+    "cs": ("sbuf", [128, 3 * 256], "uint8"),
+    "lq": ("sbuf", [128, 3 * 256], "float8_e4m3fn_x4"),
+    "ls": ("sbuf", [128, 3 * 256], "uint8"),
+    "ab": ("sbuf", [128, 5 * IT], "float32"),
     "yt": ("sbuf", [128, 1024], "float32"),
-    "cht": ("sbuf", [32, 32], "float32"),
-    "chu": ("sbuf", [32, 32], "float32"),
-    "cho": ("sbuf", [32, 8], "float32"),
-    "nx": ("sbuf", [128, 1], "float32"),
-    "nb": ("dram", [1, 128, 1], "float32"),
-    "nl": ("dram", [NR, 128, 1], "float32"),
+    "nx": ("sbuf", [128, 4], "float32"),
+    "row": ("sbuf", [1, 64], "float32"),
     "sc0": ("psum", [128, 512], "float32"),
     "sc1": ("psum", [128, 512], "float32"),
     "tr": ("psum", [128, 512], "float32"),
@@ -54,14 +54,8 @@ SCRATCH = {
     "y2": ("psum", [128, 512], "float32"),
     "y3": ("psum", [128, 512], "float32"),
 }
-SEMAPHORES = (
-    ["ldq", "ldx", "kone", "ms", "mz", "kz", "kid", "kpm", "eqd", "wqd", "xqd", "rs", "rq", "lsem", "pa", "pf", "nm", "nx",
-     "nz", "nd", "ct", "sc", "sy", "fa0", "fa1", "fa2", "fb", "fg", "ch1", "ch2", "ch3"]
-    + ["dm%d" % b for b in range(4)]
-    + ["%s%d" % (k, b) for b in range(4) for k in ("mma", "mmb", "saa", "sab", "trd", "s2", "ltd", "cb", "bcd", "obd", "ofd")]
-    + ["%s%d" % (k, i) for i in range(NI) for k in ("gx", "gr", "qz", "fm", "fy")]
-    + ["w%d" % r for r in range(NR)] + ["c%d" % r for r in range(NR)] + ["hc%d" % i for i in range(NI)]
-)
+SEMAPHORES = (["lsem", "w1", "w2"] + ["a%d" % i for i in range(16)] + ["c%d" % i for i in range(3)]
+              + ["n%d" % i for i in range(4)] + ["u%d" % i for i in range(120)])
 
 
 def rank_program(g, core, T, topo):
@@ -80,361 +74,426 @@ def rank_program(g, core, T, topo):
             place[groups[k][j]] = (k, j)
     step = sorted(range(1, ng), key=lambda d: topo.same_plane(chips[0], chips[d]))
 
-    def same(r, s):
-        return place[r][1] == place[s][1]
+    def mate_of(r):
+        return groups[place[r][0]][1 - place[r][1]]
 
     def peer_of(r):
-        k, j = place[r]
-        return groups[(k + step[-1]) % ng][j]
+        return groups[(place[r][0] + step[-1]) % ng][place[r][1]]
 
-    def sources(r, b):
-        return sorted([s for s in groups[(place[r][0] - step[b]) % ng] if s != peer_of(r)], key=lambda s: same(r, s))
-
-    def owners(r, b):
-        return [s for s in groups[(place[r][0] + step[b]) % ng] if s != peer_of(r)]
-
-    def relayed(b, r, s):
-        return b < NB - 1 and not same(r, s)
-
-    def helper_of(r):
+    def spare(r, other_die, free):
         own = cores[r]
-        far = [c for c in topo.cores_of(own) if topo.die(c) != topo.die(own) and T.rank_of(c) is None
-               and all(topo.may_write(c, t) for t in cores)]
-        return far[place[r][1]]
+        return [c for c in topo.cores_of(own) if T.rank_of(c) is None and (topo.die(c) != topo.die(own)) == other_die
+                and all(topo.may_write(c, t) for t in cores) == free][place[r][1]]
+
+    def chooser(r):
+        return spare(r, True, True)
+
+    def relays(k):
+        return sorted([c for c in range(NCORES) if topo.mates(topo.chip(c), chips[k]) and topo.may_write(c, cores[groups[k][0]])],
+                      key=topo.die)
+
+    onward, lands = {}, {}
+
+    def edge(a, piece, b):
+        if b not in onward.setdefault((a, piece), []):
+            onward[(a, piece)].append(b)
+            lands.setdefault(b, []).append(piece)
+
+    for part, c0 in (("x", 0), ("R", IT)):
+        for s in range(len(cores)):
+            k, j = place[s]
+            if part == "x":
+                edge(cores[s], (s, 0, IT), chooser(s))
+            for d in range(2):
+                to = groups[(k + step[d]) % ng]
+                way = OPT["route"][(part, d)]
+                halves = OPT["split"] and way == "b"
+                for h in range(2 if halves else 1):
+                    piece = (s, c0 + 128 * h, c0 + 128 * h + 128) if halves else (s, c0, c0 + IT)
+                    at = cores[s]
+                    if way[0] in "cg":
+                        nxt = chooser(s) if way[0] == "c" else spare(s, True, False)
+                        edge(at, piece, nxt)
+                        at = nxt
+                    if way[-1] == "b":
+                        rl = relays((k + step[d]) % ng)
+                        nxt = rl[2 * h + j] if halves else rl[2 * j + (part == "R" and OPT.get("sep", False))]
+                        edge(at, piece, nxt)
+                        at = nxt
+                    if way[-1] == "a":
+                        nxt = spare(to[j], False, False)
+                        edge(at, piece, nxt)
+                        at = nxt
+                    if way[-1] == "r":
+                        edge(at, piece, cores[to[j]])
+                        edge(cores[to[j]], piece, cores[to[1 - j]])
+                    else:
+                        for t in (to[j], to[1 - j]):
+                            edge(at, piece, cores[t])
+
+    def slot(c, s):
+        r = T.rank_of(c)
+        if r is None:
+            return 2 * IT * sorted(set(p[0] for p in lands[c])).index(s)
+        return 2 * IT * (2 * [(place[r][0] - step[d]) % ng for d in range(2)].index(place[s][0]) + place[s][1])
 
     queue = {"g": g, "v": g.vector, "s": g.scalar, "t": g.tensor, "y": g.sync}
-    cnt, seen, top = {}, {}, {}
+    cnt, seen, top, pool = {}, {}, {}, [0]
 
-    def inc(ins, name, k=1):
+    def inc(ins, name=None, k=1):
+        if name is None:
+            name = "u%d" % pool[0]
+            pool[0] += 1
         ins.then_inc(T.sem[name], k)
         cnt[name] = cnt.get(name, 0) + k
+        return name
 
-    def wait(q, name):
-        v = cnt[name]
-        if seen.get((q, name), 0) < v:
-            queue[q].wait_ge(T.sem[name], v)
-            seen[(q, name)] = v
-            top[name] = max(top.get(name, 0), v)
-
-    def expect(name, k):
-        cnt[name] = cnt.get(name, 0) + k
+    def wait(q, *names):
+        for name in names:
+            v = cnt[name]
+            if seen.get((q, name), 0) < v:
+                queue[q].wait_ge(T.sem[name], v)
+                seen[(q, name)] = v
+                top[name] = max(top.get(name, 0), v)
 
     def finish():
         for name in cnt:
             if top.get(name, 0) < cnt[name]:
                 wait("g", name)
 
-    far_core = [c for c in cores if topo.chip(c) != topo.chip(core)][0]
-    offe = topo.engines(core, far_core)
+    def lanes(a, b):
+        far = [c for c in cores if topo.chip(c) != topo.chip(a) and topo.may_write(a, c)][0]
+        if topo.chip(a) != topo.chip(b):
+            return topo.engines(a, b)
+        return [e for e in topo.engines(a, b) if e not in topo.engines(a, far)]
 
-    def mask_to(dst):
-        if topo.chip(dst) != topo.chip(core):
-            return topo.mask(core, dst)
-        return sum(1 << e for e in topo.engines(core, dst) if e not in offe)
-
-    def send(dsts, src, dst, sem, mask=None):
-        m = mask_to(dsts[0]) if mask is None else mask
-        if len(dsts) == 1:
-            rid, pid, _ = topo.addr(dsts[0])
+    def send(items):
+        kinds = {}
+        for it in items:
+            kinds.setdefault(topo.chip(it[0]) == topo.chip(core), {}).setdefault(it[4], []).append(it)
+        moves = []
+        for kind in kinds.values():
+            for n, its in enumerate(kind.values()):
+                eng = lanes(core, its[0][0])
+                eng = eng[n * len(eng) // len(kind):(n + 1) * len(eng) // len(kind)]
+                moves.append((its, sum(1 << e for e in eng)))
+                cnt["lsem"] = cnt.get("lsem", 0) + len(eng)
+        if len(items) == 1:
+            to, src, dst, sem, _ = items[0]
+            rid, pid, _ = topo.addr(to)
             g.remote_dma(out_ap=dst, in_ap=src, remote_sem=T.sem[sem], local_sem=T.sem["lsem"], pid=pid,
-                         routing_id=rid, dma_engine_mask=m)
-        else:
-            ids = []
-            for d in dsts:
-                rid, pid, _ = topo.addr(d)
-                ids.append(DstId(rid=rid, pnc=pid))
-            g.remote_dma_fused([RemoteDMATransfer(dst_ids=ids, dma_engine_mask=m, remote_sem=T.sem[sem], srcs=[src],
-                                                  dsts=[dst] * len(dsts))], local_sem=T.sem["lsem"])
-        cnt["lsem"] = cnt.get("lsem", 0) + bin(m).count("1")
+                         routing_id=rid, dma_engine_mask=moves[0][1])
+            return
+        g.remote_dma_fused([RemoteDMATransfer(dst_ids=[DstId(rid=topo.addr(it[0])[0], pnc=topo.addr(it[0])[1]) for it in its],
+                                              dma_engine_mask=m, remote_sem=T.sem[its[0][3]], srcs=[its[0][1]],
+                                              dsts=[it[2] for it in its]) for its, m in moves], local_sem=T.sem["lsem"])
 
-    n_off, n_on = len(offe), len([e for e in topo.engines(core, [c for c in topo.cores_of(core) if c != core][0])
-                                  if e not in offe])
+    def send_mx(items):
+        send([(i[0], i[1][:, i[3]:i[4]].bitcast(dt.uint8), i[5][:, i[7]:i[7] + i[4] - i[3]].bitcast(dt.uint8), i[8], (i[3], i[8]))
+              for i in items])
+        send([(i[0], i[2][:, i[3]:i[4]], i[6][:, i[7]:i[7] + i[4] - i[3]], i[8], (i[3], i[8])) for i in items])
 
-    def send_xr(dst, codes, plane, codes2, plane2, sem):
-        send([dst], codes[:, :].bitcast(dt.uint8), codes2[:, :].bitcast(dt.uint8), sem)
-        send([dst], plane[:, :], plane2[:, :], sem)
+    def piece_sem(piece):
+        s, a, e = piece
+        return "a%d" % (4 * (2 * (place[s][0] // 2) + place[s][1]) + a // 128)
 
-    def send_c(dst, i, s):
-        send([dst], T.cq[:, 256 * i:256 * i + 256].bitcast(dt.uint8), T.lq[:, 256 * s:256 * s + 256].bitcast(dt.uint8), "c%d" % s)
-        send([dst], T.cs[:, 256 * i:256 * i + 256], T.ls[:, 256 * s:256 * s + 256], "c%d" % s)
+    def groups_of(a, pieces):
+        out = {}
+        for p in pieces:
+            if (a, p) in onward:
+                out.setdefault(p[2] - p[1], []).append(p)
+        return list(out.values())
 
-    rank = T.rank_of(core)
-    if rank is None:
-        for r in range(len(cores)):
-            if helper_of(r) == core:
-                expect("pa", 2 * n_on)
-                wait("g", "pa")
-                send_xr(cores[peer_of(r)], T.pq, T.ps, T.fq, T.fs, "pf")
-                for b in range(NB):
-                    for j, d in enumerate(sources(r, b)):
-                        if relayed(b, d, r):
-                            i = 2 * b + j
-                            expect("hc%d" % i, 2 * n_on)
-                            wait("g", "hc%d" % i)
-                            send_c(cores[d], i, r)
-                finish()
-        return
+    def arrivals(c):
+        for (a, p), tos in onward.items():
+            if c in tos:
+                side = [q for q in range(len(cores)) if cores[q] == a]
+                share = 1
+                if side and side[0] == p[0]:
+                    part = [q for q in all_pieces(p[0], p[1] // IT) if (a, q) in onward and q[2] - q[1] == p[2] - p[1]
+                            and any((topo.chip(t) == topo.chip(a)) == (topo.chip(c) == topo.chip(a)) for t in onward[(a, q)])]
+                    share = len(part)
+                cnt[piece_sem(p)] = cnt.get(piece_sem(p), 0) + 2 * len(lanes(a, c)) // share
 
-    m, _ = place[rank]
-    duo = groups[m]
-    mate = [r for r in duo if r != rank][0]
-    peer = peer_of(rank)
-    near = duo + [peer]
-    helper = helper_of(rank)
+    def all_pieces(s, half):
+        return sorted(set(p for (a, p) in onward if p[0] == s and p[1] // IT == half), key=lambda p: (p[1] - p[2], p[1]))
+
+    def pass_on(pieces, codes, plane, base):
+        send_mx([(t, codes, plane, base(p) + p[1], base(p) + p[2], T.aq, T["as"], slot(t, p[0]) + p[1], piece_sem(p))
+                 for p in pieces for t in onward[(core, p)]])
+
+    def forward(p):
+        wait("g", piece_sem(p))
+        pass_on([p], T.aq, T["as"], lambda q: slot(core, q[0]))
+
     v, pe, act, sy = g.vector, g.tensor, g.scalar, g.sync
     COPY = ActivationFunctionType.Copy
-    ADD, MAX = AluOpType.add, AluOpType.max
+    ADD, MAX, MUL = AluOpType.add, AluOpType.max, AluOpType.mult
+    free = {}
 
-    inc(sy.dma_start(T.qt[:, :], T.qw[:, :]), "ldq", 16)
-    inc(sy.dma_start(T.xr[:, 0:4 * IT], T.x[:, :]), "ldx", 16)
+    def take(bank):
+        wait("t", *free.get(bank.name, []))
+        free[bank.name] = []
 
-    inc(v.memset(T.onb[:, :], 1.0), "kone")
-    inc(v.memset(T.onf[:, :], 1.0), "kone")
-    inc(v.memset(T.rst[:, :], 0.0), "mz")
-    inc(v.memset(T.bc[:, :], 0.0), "ms")
-    inc(v.memset(T.neg[:, :], LOW), "ms")
-    inc(v.memset(T.cht[:, :], 0.0), "ms")
-    inc(v.memset(T.cc[:, :], 0.0), "ms")
-    wait("v", "mz")
-    inc(v.memset(T.rst[:, 0:256:16], LOW), "ms")
-    wait("g", "kone")
-    inc(g.affine_select(T.zt[:, :], T.onb[:, :], [[-1, 516]], AluOpType.is_equal, 0.0, 3, 4), "kz")
-    inc(g.affine_select(T.ident[:, :], T.onf[:, :], [[-1, 128]], AluOpType.is_equal, 0.0, 0, 1), "kid")
+    def constants():
+        one = inc(v.memset(T.onf[:, :], 1.0))
+        z = inc(v.memset(T.rst[:, :], 0.0))
+        ms = inc(v.memset(T.neg[:, :], LOW))
+        inc(v.memset(T.cc[:, :], 0.0), ms)
+        wait("v", z)
+        inc(v.memset(T.rst[:, 0:256:16], LOW), ms)
+        wait("g", one)
+        kid = inc(g.affine_select(T.ident[:, :], T.onf[:, :], [[-1, 128]], AluOpType.is_equal, 0.0, 0, 1))
+        return ms, kid
 
-    wait("v", "ldq")
-    w0 = Q * rank
-    wcols = T.wq[:, w0:w0 + Q], T.ws[:, w0:w0 + Q]
-    inc(v.quantize_mx(wcols[0], wcols[1], T.qt[:, :]), "wqd")
-    wait("g", "wqd")
-    for b in range(NB):
-        to = [cores[s] for s in owners(rank, b)]
-        send(to, wcols[0].bitcast(dt.uint8), wcols[0].bitcast(dt.uint8), "w%d" % rank)
-        send(to, wcols[1], wcols[1], "w%d" % rank)
+    def scores(bank, codes, plane, c0, w0, n):
+        take(bank)
+        return inc(pe.matmul_mx(bank[:, 0:n], codes[:, c0:c0 + 128], plane[:, c0:c0 + 128], T.wq[:, w0:w0 + n], T.ws[:, w0:w0 + n], True, True))
 
-    wait("v", "ldx")
-    inc(v.quantize_mx(T.xq[:, 0:IT], T.xs[:, 0:IT], T.xr[:, 0:4 * IT]), "xqd")
-    wait("v", "kz")
-    for b in range(4):
-        inc(v.quantize_mx(T.eq[:, 128 * b:128 * b + 128], T.es[:, 128 * b:128 * b + 128], T.zt[:, 3 - b:3 - b + 512]), "eqd")
-    wait("t", "xqd")
-    wait("t", "eqd")
-    ybank = [T.y0, T.y1, T.y2, T.y3]
-    for b in range(4):
-        inc(pe.matmul_mx(ybank[b][:, 0:IT], T.eq[:, 128 * b:128 * b + 128], T.es[:, 128 * b:128 * b + 128],
-                         T.xq[:, 0:IT], T.xs[:, 0:IT], True, True), "dm%d" % b)
-    for b in range(4):
-        wait("v", "dm%d" % b)
-        inc(v.tensor_tensor(T.xr[:, 4 * IT + b:8 * IT:4], T.xr[:, b:4 * IT:4], ybank[b][:, 0:IT], AluOpType.subtract), "rs")
-    wait("v", "rs")
-    inc(v.quantize_mx(T.xq[:, IT:2 * IT], T.xs[:, IT:2 * IT], T.xr[:, 4 * IT:8 * IT]), "rq")
-    wait("g", "rq")
-    for to in (helper, cores[mate]):
-        send_xr(to, T.xq, T.xs, T.pq, T.ps, "pa")
-    inc(g.iota(T.pm[:, :], [[0, 8], [1, 16]], 0, 0, allow_small_or_imprecise_dtypes=True), "kpm")
+    def over_queries(bank, done, at, n, sem=None):
+        wait("v", done)
+        sem = inc(v.tensor_tensor_scan(T.S[:, at:at + n], T.rst[:, 0:n], bank[:, 0:n], 0.0, ADD, MAX), sem)
+        free[bank.name] = [sem]
+        return sem
 
-    wait("y", "ms")
-    inc(sy.dma_start(T.nb[0:1, :, 0], T.bc[64:65, 0:128]), "nz", 16)
-    wait("y", "nz")
+    def over_items(b, at, k, halves):
+        take(T.tr)
+        done = None
+        for h in range(2):
+            wait("t", *halves[h])
+            a = at + 16 * k * h
+            done = inc(pe.transpose(T.tr[0:k, 128 * h:128 * h + 128], T.S[:, a + 15:a + 16 * k:16], T.ident[:, :]), done)
+        p = 256 * b
+        wait("v", done)
+        s2 = inc(v.tensor_tensor_scan(T.P[0:k, p:p + 256], T.tr[0:k, 0:256], T.neg[0:k, :], LOW, MAX, MAX))
+        free["tr"] = [s2]
+        wait("v", s2)
+        lt = inc(v.tensor_scalar(T.lt[0:k, 16 * b:16 * b + 16], T.P[0:k, p + 15:p + 256:16], T.P[0:k, p + 255:p + 256], None, AluOpType.is_lt))
+        wait("v", lt)
+        return inc(v.tensor_reduce(T.cc[0:k, 4 * b:4 * b + 1], T.lt[0:k, 16 * b:16 * b + 16], AxisListType.X, ADD))
 
-    own = {rank: (T.xq, T.xs), mate: (T.pq, T.ps), peer: (T.fq, T.fs)}
-    banks = {rank: (T.sc0, T.sc1), mate: (T.y0, T.y1), peer: (T.y2, T.y3)}
-
-    def width(b):
-        return len(near) if b == NB else len(sources(rank, b))
-
-    def products(b):
-        if b < NB:
-            src = sources(rank, b)
-            for r in src:
-                expect("w%d" % r, 2 * n_off)
-                wait("t", "w%d" % r)
-            c0, n = Q * min(src), Q * len(src)
-            for h in range(2):
-                if b:
-                    wait("t", ("saa%d", "sab%d")[h] % (b - 1))
-                inc(pe.matmul_mx(banks[rank][h][:, 0:n], T.xq[:, 128 * h:128 * h + 128], T.xs[:, 128 * h:128 * h + 128],
-                                 T.wq[:, c0:c0 + n], T.ws[:, c0:c0 + n], True, True), ("mma%d", "mmb%d")[h] % b)
+    rank = T.rank_of(core)
+    arrivals(core)
+    if rank is None:
+        if core not in lands:
             return
-        expect("pa", 2 * n_on)
-        expect("pf", 2 * n_off)
-        for f in ("rs", "wqd", "rq", "saa%d" % (b - 1), "sab%d" % (b - 1)):
-            wait("t", f)
-        for s in (rank, mate, peer):
-            if s != rank:
-                wait("t", "pa" if s == mate else "pf")
+        jobs = sorted([p for p in lands[core] if (core, p) in onward], key=lambda p: p[1])
+        mine = [r for r in range(len(cores)) if chooser(r) == core]
+        for p in jobs:
+            if p[1] < IT:
+                forward(p)
+        if mine:
+            s = mine[0]
+            far = mate_of(peer_of(s))
+            ms, kid = constants()
+            cnt["w1"] = 2 * len(lanes(cores[far], core))
+            cnt["w2"] = 2 * len(lanes(cores[s], core))
+            wait("t", kid, piece_sem((s, 0, IT)), "w1", "w2")
+            wait("v", ms)
+            halves = []
             for h in range(2):
-                inc(pe.matmul_mx(banks[s][h][:, 0:128], own[s][0][:, 128 * h:128 * h + 128], own[s][1][:, 128 * h:128 * h + 128],
-                                 wcols[0], wcols[1], True, True), ("mma%d", "mmb%d")[h] % b)
+                bank = (T.sc0, T.sc1)[h]
+                halves.append([over_queries(bank, scores(bank, T.aq, T["as"], 128 * h, Q, 2 * Q), 256 * h, 256)])
+            wait("g", over_items(0, 0, 16, halves))
+            col = T.cc[:, 0:1]
+            send([(cores[s], col, T.nx[:, 0:1], "n0", 0), (cores[far], col, T.nx[:, 2:3], "n2", 1)])
+            send([(cores[mate_of(s)], col, T.nx[:, 3:4], "n3", 0)])
+        for p in jobs:
+            if p[1] >= IT:
+                forward(p)
+        finish()
+        return
 
-    def over_queries(b):
-        o, n = 512 * b, 128 * width(b)
-        wait("v", "ms")
-        for h in range(2):
-            wait("v", ("mma%d", "mmb%d")[h] % b)
-            parts = [(n, banks[rank][h], 0)] if b < NB else [(128, banks[s][h], 128 * l) for l, s in enumerate(near)]
-            for w, bank, at in parts:
-                q = o + n * h + at
-                inc(v.tensor_tensor_scan(T.S[:, q:q + w], T.rst[:, 0:w], bank[:, 0:w], 0.0, ADD, MAX), ("saa%d", "sab%d")[h] % b)
-        wait("t", "kid")
-        if b:
-            wait("t", "s2%d" % (b - 1))
-        for h in range(2):
-            wait("t", ("saa%d", "sab%d")[h] % b)
-            inc(pe.transpose(T.tr[0:n // 16, 128 * h:128 * h + 128], T.S[:, o + n * h + 15:o + n * h + n:16], T.ident[:, :]), "trd%d" % b)
+    mate, peer = mate_of(rank), peer_of(rank)
+    other = mate_of(peer)
+    whole = [groups[(place[rank][0] - step[d]) % ng] for d in range(2)]
+    wcols = T.wq[:, 0:Q], T.ws[:, 0:Q]
+    n_on, n_off = len(lanes(core, cores[mate])), len(lanes(core, cores[peer]))
+    for name, k in (("w1", 2 * n_off), ("c0", 2 * n_off), ("c1", 2 * n_off), ("c2", 2 * n_on), ("n0", n_on), ("n1", n_off),
+                    ("n2", n_off), ("n3", n_on)):
+        cnt[name] = k
 
-    def over_items(b):
-        p, k = 256 * b, 8 * width(b)
-        wait("v", "trd%d" % b)
-        inc(v.tensor_tensor_scan(T.P[0:k, p:p + 256], T.tr[0:k, 0:256], T.neg[0:k, :], LOW, MAX, MAX), "s2%d" % b)
-        wait("v", "s2%d" % b)
-        inc(v.tensor_scalar(T.lt[0:k, 16 * b:16 * b + 16], T.P[0:k, p + 15:p + 256:16], T.P[0:k, p + 255:p + 256], 64.0,
-                            AluOpType.is_lt, AluOpType.mult), "ltd%d" % b)
-        wait("v", "ltd%d" % b)
-        col = T.cc[0:k, 4 * b:4 * b + 1]
-        inc(v.tensor_reduce(col, T.lt[0:k, 16 * b:16 * b + 16], AxisListType.X, ADD), "cb%d" % b)
-        wait("v", "cb%d" % b)
-        wait("v", "kpm")
-        if b < NB:
-            inc(v.tensor_scalar(T.bc[0:k, 128 * b:128 * b + 128], T.pm[0:k, :], col, None, ADD), "bcd%d" % b)
-            if b < NB - 1:
-                wait("y", "cb%d" % b)
-                q = 8 * min(sources(rank, b))
-                inc(sy.dma_start(T.nb[0:1, q:q + k, 0], col), "nd", 16)
-        else:
-            inc(v.tensor_scalar(T.bc[0:k, 128 * b:128 * b + 128], T.pm[0:k, :], 4.0, col, AluOpType.mult, ADD), "bcd%d" % b)
-        wait("t", "bcd%d" % b)
-        if b:
-            wait("t", "ofd%d" % (b - 1))
-        inc(pe.transpose(T.ob[:, 0:128], T.bc[:, 128 * b:128 * b + 128], T.ident[:, :]), "obd%d" % b)
+    ldq = inc(sy.dma_start(T.qt[:, :], T.qw[:, :]), None, 16)
+    ldx = inc(act.dma_start(T.xr[:, 0:4 * IT], T.x[:, :]), None, 16)
+    kone = inc(v.memset(T.onb[:, :], 1.0))
+    wait("g", kone)
+    kz = inc(g.affine_select(T.zt[:, :], T.onb[:, :], [[-1, 516]], AluOpType.is_equal, 0.0, 3, 4))
+    ms, kid = constants()
+    kpm = inc(g.iota(T.pm[:, :], [[0, 8], [1, 16]], 0, 0, allow_small_or_imprecise_dtypes=True))
+    inc(v.memset(T.bc[:, :], 0.0), ms)
+    un = inc(v.memset(T.unit[:, :], 1.0 / 64.0))
+    wait("v", un)
+    inc(v.memset(T.unit[0:8, :], 1.0 / 16.0), ms)
+    wait("v", kz)
+    eqd = None
+    for b in range(4):
+        eqd = inc(v.quantize_mx(T.eq[:, 128 * b:128 * b + 128], T.es[:, 128 * b:128 * b + 128], T.zt[:, 3 - b:3 - b + 512]), eqd)
 
-    def offsets(b):
-        k = 8 * width(b)
-        wait("v", "obd%d" % b)
-        if b < NB:
-            for u in range(4):
-                inc(v.tensor_scalar(T.of[:, 64 * b + u:64 * b + 4 * k:4], T.ob[:, 0:k], float(16 * u), None, ADD), "ofd%d" % b)
-        else:
-            inc(v.tensor_scalar(T.of[:, 64 * b:64 * b + k], T.ob[:, 0:k], 0.25, None, AluOpType.mult), "ofd%d" % b)
-        wait("v", "ofd%d" % b)
+    wait("v", ldq)
+    wqd = inc(v.quantize_mx(wcols[0], wcols[1], T.qt[:, :]))
+    wait("g", wqd)
+    for to in (chooser(other), cores[peer]):
+        send_mx([(to, T.wq, T.ws, 0, Q, T.wq, T.ws, Q, "w1")])
 
-    def lists(b, j):
-        src = sources(rank, b)
-        return 64 * b + 32 * sorted(src).index(src[j])
+    wait("v", ldx)
+    xqd = inc(v.quantize_mx(T.xq[:, 0:IT], T.xs[:, 0:IT], T.xr[:, 0:4 * IT]))
+    wait("g", xqd)
+    for ps in groups_of(core, all_pieces(rank, 0)):
+        pass_on(ps, T.xq, T.xs, lambda p: 0)
+        if ps[0][2] - ps[0][1] == IT:
+            send_mx([(chooser(mate), T.wq, T.ws, 0, Q, T.wq, T.ws, 2 * Q, "w2")])
+    wait("t", xqd, eqd)
+    ybank = [T.y0, T.y1, T.y2, T.y3]
+    dm = [inc(pe.matmul_mx(ybank[b][:, 0:IT], T.eq[:, 128 * b:128 * b + 128], T.es[:, 128 * b:128 * b + 128],
+                           T.xq[:, 0:IT], T.xs[:, 0:IT], True, True)) for b in range(4)]
+    rs = None
+    for b in range(4):
+        wait("v", dm[b])
+        rs = inc(v.tensor_tensor(T.xr[:, 4 * IT + b:8 * IT:4], T.xr[:, b:4 * IT:4], ybank[b][:, 0:IT], AluOpType.subtract), rs)
+        free[ybank[b].name] = [rs]
+    wait("v", rs)
+    rq = inc(v.quantize_mx(T.xq[:, IT:2 * IT], T.xs[:, IT:2 * IT], T.xr[:, 4 * IT:8 * IT]))
+    wait("g", rq)
+    for ps in groups_of(core, all_pieces(rank, 1)):
+        pass_on(ps, T.xq, T.xs, lambda p: 0)
 
-    def gather_x(b, j, q, a, e):
-        i, f = 2 * b + j, lists(b, j)
-        out, win = T.gt[:, 1024 * i + a:1024 * i + e], T.xr[:, 0:1024].indirect(T.of[:, f + a // 16:f + e // 16])
-        wait(q, "ofd%d" % b)
-        inc(v.tensor_copy(out, win) if q == "v" else act.activation(out, win, COPY), "gx%d" % i if q == "v" else "gr%d" % i)
+    def landed(q, s, half):
+        wait(q, *[piece_sem(p) for p in lands[core] if p[0] == s and p[1] // IT == half])
 
-    def gather_r(b, j):
-        i, f = 2 * b + j, lists(b, j)
-        wait("s", "ofd%d" % b)
-        wait("s", "rs")
-        inc(act.activation(T.gt[:, 1024 * i + 512:1024 * i + 1024], T.xr[:, 1024:2048].indirect(T.of[:, f:f + 32]), COPY), "gr%d" % i)
+    def both(bank, codes, plane, c0, n, l):
+        take(bank)
+        pe.matmul_mx(bank[:, 0:n], wcols[0], wcols[1], codes[:, c0:c0 + n], plane[:, c0:c0 + n], True, False)
+        done = inc(pe.matmul_mx(bank[:, 0:n], wcols[0], wcols[1], codes[:, c0 + n:c0 + 2 * n], plane[:, c0 + n:c0 + 2 * n], False, True))
+        wait("s", done)
+        out = inc(act.activation(l, bank[:, 0:n], COPY))
+        free[bank.name] = [out]
+        return out
 
-    def pack(b, j):
-        i = 2 * b + j
-        wait("v", "gx%d" % i)
-        wait("v", "gr%d" % i)
-        inc(v.quantize_mx(T.cq[:, 256 * i:256 * i + 256], T.cs[:, 256 * i:256 * i + 256], T.gt[:, 1024 * i:1024 * i + 1024]), "qz%d" % i)
+    def spread(b, col, k, done, unit):
+        wait("v", done, kpm)
+        bcd = inc(v.tensor_scalar(T.bc[0:k, 128 * b:128 * b + 128], T.pm[0:k, :], unit, col, MUL, ADD))
+        take(T.ob)
+        wait("t", bcd)
+        obd = inc(pe.transpose(T.ob[:, 128 * b:128 * b + 128], T.bc[:, 128 * b:128 * b + 128], T.ident[:, :]))
+        wait("v", obd)
 
-    def ship(b, j):
-        i, d = 2 * b + j, sources(rank, b)[j]
-        wait("g", "qz%d" % i)
-        if relayed(b, d, rank):
-            send([helper], T.cq[:, 256 * i:256 * i + 256].bitcast(dt.uint8), T.cq[:, 256 * i:256 * i + 256].bitcast(dt.uint8), "hc%d" % i)
-            send([helper], T.cs[:, 256 * i:256 * i + 256], T.cs[:, 256 * i:256 * i + 256], "hc%d" % i)
-        else:
-            send_c(cores[d], i, rank)
+    def lists(f, c0, k):
+        sem = None
+        for u in range(4):
+            sem = inc(v.tensor_scalar(T.of[:, f + u:f + 4 * k:4], T.ob[:, c0:c0 + k], 64.0, float(16 * u), MUL, ADD), sem)
+        free["ob"] = free.get("ob", []) + [sem]
+        return sem
 
-    products(0)
-    over_queries(0)
-    over_items(0)
-    offsets(0)
-    for b in range(NB):
-        last = b == NB - 1
-        items = range(width(b))
-        for j in items:
-            gather_r(b, j)
-        if not last:
-            gather_x(b, 1, "s", 256, 512)
-        gather_x(b, 0, "v", 0, 512)
-        if not last:
-            products(b + 1)
-            over_queries(b + 1)
-        pack(b, 0)
-        if not last:
-            gather_x(b, 1, "v", 0, 256)
-            pack(b, 1)
-            over_items(b + 1)
-            offsets(b + 1)
-        for j in items:
-            ship(b, j)
-        if b == NB - 2:
-            wait("g", "nd")
-            send([cores[o] for k in range(NB - 1) for o in sources(rank, k)], T.nb[0], T.nl[rank], "nm", 1 << offe[-1])
-            wait("g", "cb%d" % (NB - 1))
-            send([cores[sources(rank, NB - 1)[0]]], T.cc[:, 4 * NB - 4:4 * NB - 3], T.nx[:, :], "nx")
+    def tile(i, f, ofd, to):
+        a, vx = 1024 * i, OPT["vx"]
+        wait("s", ofd, rs)
+        gr = inc(act.activation(T.gt[:, a + 512:a + 1024], T.xr[:, 1024:2048].indirect(T.of[:, f:f + 32]), COPY))
+        if vx < 512:
+            inc(act.activation(T.gt[:, a + vx:a + 512], T.xr[:, 0:1024].indirect(T.of[:, f + vx // 16:f + 32]), COPY), gr)
+        wait("v", ofd)
+        gx = inc(v.tensor_copy(T.gt[:, a:a + vx], T.xr[:, 0:1024].indirect(T.of[:, f:f + vx // 16])))
+        wait("v", gx, gr)
+        qz = inc(v.quantize_mx(T.cq[:, 256 * i:256 * i + 256], T.cs[:, 256 * i:256 * i + 256], T.gt[:, a:a + 1024]))
+        wait("g", qz)
+        send_mx([(cores[to], T.cq, T.cs, 256 * i, 256 * i + 256, T.lq, T.ls, 256 * i, "c%d" % i)])
 
-    order = [(T.y1, "sab%d" % NB), (T.y2, "saa%d" % NB), (T.y3, "sab%d" % NB), (T.y0, "fb")]
-    tiles = [(b, s) for b in range(NB) for s in owners(rank, b)]
-    tiles.sort(key=lambda e: (2 + 2 * e[0]) if relayed(e[0], e[1], rank) else (0, 1, 3)[e[0]])
+    stores = []
 
-    def final(l):
-        for p in l:
-            s = tiles[p][1]
-            bank = order[p % 4][0]
-            expect("c%d" % s, 2 * n_off)
-            wait("t", order[p][1] if p < 4 else "fy%d" % (p - 4))
-            wait("t", "c%d" % s)
-            pe.matmul_mx(bank[:, 0:128], wcols[0], wcols[1], T.lq[:, 256 * s:256 * s + 128], T.ls[:, 256 * s:256 * s + 128], True, False)
-            inc(pe.matmul_mx(bank[:, 0:128], wcols[0], wcols[1], T.lq[:, 256 * s + 128:256 * s + 256],
-                             T.ls[:, 256 * s + 128:256 * s + 256], False, True), "fm%d" % p)
-            wait("s", "fm%d" % p)
-            inc(act.activation(T.yt[:, 128 * s:128 * s + 128], bank[:, 0:128], COPY), "fy%d" % p)
-            wait("s", "fy%d" % p)
-            inc(act.dma_start(T.y[:, 128 * s:128 * s + 128], T.yt[:, 128 * s:128 * s + 128]), "sy", 16)
+    def store(s, n, done):
+        wait("y", *done)
+        stores.append(inc(sy.dma_start(T.y[:, 128 * s:128 * (s + n)], T.yt[:, 128 * s:128 * (s + n)]), None, 16))
 
-    b = NB
-    products(b)
-    over_queries(b)
-    wide = (T.sc0, T.sc1, T.y0)
-    for l, s in enumerate(near):
-        wait("t", ("saa%d" if l != 1 else "sab%d") % b)
-        pe.matmul_mx(wide[l][:, 0:IT], wcols[0], wcols[1], own[s][0][:, 0:IT], own[s][1][:, 0:IT], True, False)
-        inc(pe.matmul_mx(wide[l][:, 0:IT], wcols[0], wcols[1], own[s][0][:, IT:2 * IT], own[s][1][:, IT:2 * IT], False, True), "fa%d" % l)
-        wait("s", "fa%d" % l)
-        inc(act.activation(T.ab[:, IT * l:IT * l + IT], wide[l][:, 0:IT], COPY), "fb")
-    final(range(0, 2))
-    over_items(b)
-    wait("y", "cb%d" % b)
-    inc(sy.dma_start(T.cht[duo[0]:duo[0] + 2, 0:8], T.cc[0:16, 4 * b:4 * b + 1]), "ct", 16)
-    inc(sy.dma_start(T.cht[peer:peer + 1, 0:8], T.cc[16:24, 4 * b:4 * b + 1]), "ct", 16)
-    offsets(b)
-    wait("v", "fb")
-    for l, s in enumerate(near):
-        f0 = 64 * b + 8 * l
-        inc(v.tensor_copy(T.yt[:, 128 * s:128 * s + 128], T.ab[:, IT * l:IT * l + IT].indirect(T.of[:, f0:f0 + 8])), "fg")
-    wait("s", "fg")
-    inc(act.dma_start(T.y[:, 128 * duo[0]:128 * duo[0] + 256], T.yt[:, 128 * duo[0]:128 * duo[0] + 256]), "sy", 16)
-    inc(act.dma_start(T.y[:, 128 * peer:128 * peer + 128], T.yt[:, 128 * peer:128 * peer + 128]), "sy", 16)
-    final(range(2, NI))
+    wait("t", wqd, kid)
+    wait("v", ms)
+    halves = [[over_queries((T.sc0, T.sc1)[h], scores((T.sc0, T.sc1)[h], T.xq, T.xs, 128 * h, 0, Q), 256 * h, Q)] for h in range(2)]
+    wait("t", rq)
+    st = {"ab": [both(T.y2, T.xq, T.xs, 0, IT, T.ab[:, 0:IT])], "near": [[], []]}
+    wait("t", "w1")
+    for h in range(2):
+        halves[h].append(over_queries(ybank[h], scores(ybank[h], T.xq, T.xs, 128 * h, Q, Q), 256 * h + Q, Q))
+    first = over_items(0, 0, 16, halves)
+    spread(0, T.cc[0:16, 0:1], 16, first, T.unit[0:16, :])
+    of1 = lists(0, 8, 8)
+    of0 = inc(v.tensor_scalar(T.of[:, 32:40], T.ob[:, 0:8], 16.0, None, MUL))
+    free["ob"].append(of0)
 
-    expect("nm", sum(len(owners(rank, k)) for k in range(NB - 1)))
-    expect("nx", n_off)
-    wait("y", "nm")
-    for k in range(NB - 1):
-        s = owners(rank, k)[0]
-        inc(sy.dma_start(T.cht[s:s + 2, 0:8], T.nl[s:s + 2, 8 * rank:8 * rank + 8, 0]), "ct", 16)
-    wait("v", "ct")
-    inc(v.transpose(T.chu[:, :], T.cht[:, :]), "ch1")
-    wait("v", "ch1")
-    inc(v.tensor_scalar(T.cho[0:8, 0:8], T.chu[0:8, 0:8], 1.0 / 64.0, None, AluOpType.mult), "ch2")
-    wait("v", "ch2")
-    wait("v", "nx")
-    s = owners(rank, NB - 1)[0]
-    inc(v.tensor_scalar(T.cho[0:8, s:s + 1], T.nx[0:8, :], 1.0 / 64.0, None, AluOpType.mult), "ch3")
-    wait("y", "ch3")
-    inc(sy.dma_start(T.ch[:, :], T.cho[0:8, 0:8]), "sc", 16)
+    def t1():
+        tile(0, 0, of1, peer)
+        wait("g", first)
+        send([(cores[peer], T.cc[:, 0:1], T.nx[:, 1:2], "n1", 0)])
+        wait("v", of0, st["ab"][0])
+        store(rank, 1, [inc(v.tensor_copy(T.yt[:, 128 * rank:128 * rank + 128], T.ab[:, 0:IT].indirect(T.of[:, 32:40])))])
+
+    def near(d):
+        banks = ((T.sc0, T.sc1, T.y2, T.y3), (T.y0, T.y1, T.sc0, T.sc1))[d]
+        for j, s in enumerate(whole[d]):
+            landed("t", s, 0)
+            for h in range(2):
+                bank = banks[2 * j + h]
+                done = scores(bank, T.aq, T["as"], slot(core, s) + 128 * h, 0, Q)
+                st["near"][h].append(over_queries(bank, done, 512 + 512 * h + 128 * (2 * d + j), Q))
+
+    def fwd():
+        for p in lands[core]:
+            if (core, p) in onward:
+                forward(p)
+
+    def num():
+        spread(1, T.nx[0:16, 0:1], 16, "n0", 1.0 / 64.0)
+        st["of"] = lists(64, 128, 16)
+
+    def ab(d):
+        for j, s in enumerate(whole[d]):
+            landed("t", s, 0)
+            landed("t", s, 1)
+            l = 1 + 2 * d + j
+            st["ab"].append(both(((T.y2, T.y3), (T.y0, T.y1))[d][j], T.aq, T["as"], slot(core, s), IT, T.ab[:, IT * l:IT * l + IT]))
+
+    def fin(i):
+        s = (peer, other, mate)[i]
+        wait("t", "c%d" % i)
+        store(s, 1, [both((T.sc0, T.sc1, T.sc0)[i], T.lq, T.ls, 256 * i, 128, T.yt[:, 128 * s:128 * s + 128])])
+
+    def pick():
+        done = over_items(1, 512, 32, st["near"])
+        spread(2, T.cc[0:32, 4:5], 32, done, 1.0 / 16.0)
+        sem = None
+        for l in range(4):
+            sem = inc(v.tensor_scalar(T.of[:, 128 + 8 * l:136 + 8 * l], T.ob[:, 256 + 8 * l:264 + 8 * l], 16.0, float(IT * (l % 2)), MUL, ADD), sem)
+        st["ofn"] = sem
+        free["ob"].append(sem)
+        src = {rank: T.ob[0:1, 0:8], peer: T.ob[0:1, 392:400], other: T.tr[0:1, 256:264], mate: T.tr[0:1, 392:400]}
+        for l, s in enumerate(whole[0] + whole[1]):
+            src[s] = T.ob[0:1, 256 + 8 * l:264 + 8 * l]
+        st["src"] = src
+
+    def rows():
+        sem = None
+        take(T.tr)
+        take(T.ob)
+        for n, out in ((1, T.ob[0:1, 384:512]), (2, T.tr[0:1, 256:384]), (3, T.tr[0:1, 384:512])):
+            wait("t", "n%d" % n)
+            sem = inc(pe.transpose(out, T.nx[:, n:n + 1], T.ident[:, :]), sem)
+        st["rows"] = sem
+
+    def last():
+        for d in range(2):
+            q = "vs"[d]
+            s = whole[d][0]
+            wait(q, st["ofn"], st["ab"][1 + 2 * d], st["ab"][2 + 2 * d])
+            out, win = T.yt[:, 128 * s:128 * s + 256], T.ab[:, IT * (1 + 2 * d):IT * (3 + 2 * d)].indirect(T.of[:, 128 + 16 * d:144 + 16 * d])
+            store(s, 2, [inc(v.tensor_copy(out, win) if q == "v" else act.activation(out, win, COPY))])
+        sem = None
+        wait("v", st["rows"])
+        for s in range(NR):
+            sem = inc(v.tensor_copy(T.row[0:1, s:64:8], st["src"][s]), sem)
+        wait("s", sem)
+        inc(act.dma_start(T.ch[:, :], T.row[0:1, :]), None, 16)
+
+    steps = {"t1": t1, "near0": lambda: near(0), "near1": lambda: near(1), "fwd": fwd, "num": num,
+             "t2": lambda: tile(1, 64, st["of"], other), "t3": lambda: tile(2, 96, st["of"], mate),
+             "ab0": lambda: ab(0), "ab1": lambda: ab(1), "fin1": lambda: fin(0), "fin2": lambda: fin(1), "fin3": lambda: fin(2),
+             "pick": pick, "rows": rows, "last": last}
+    for name in OPT["order"]:
+        steps[name]()
     finish()

@@ -1,14 +1,17 @@
 from concourse.bass import DstId, RemoteDMATransfer
-from concourse.mybir import dt, AluOpType, ActivationFunctionType, AxisListType
+from concourse.mybir import dt, AluOpType, ActivationFunctionType
 
 NR, Q, IT = 8, 128, 256
 LOW = -5.0e29
 NCORES = 128
 OPT = {
-    "route": {("x", 0): "cr", ("R", 0): "c", ("x", 1): "b", ("R", 1): "b"},
-    "split": True,
-    "vx": 384,
-    "order": ["t1", "fwd", "num", "t2", "t3", "near0", "near1", "fin1", "pick", "fin3", "fin2", "ab0", "ab1", "rows", "last"],
+    "route": {("x", 0): "r", ("R", 0): "c", ("x", 1): "cr", ("R", 1): "b"},
+    "split": True, "sep": False, "seq": True, "via": "", "fuseq": 0,
+    "vx": [512, 512, 448],
+    "parts": [1, 1, 1],
+    "own": "s",
+    "order": ["fx0", "fx1", "num", "g1", "num2", "p1", "g2", "tell", "p2", "g3", "own", "p3", "near0", "near1", "pick", "fR1",
+              "ab0", "fin1", "place", "ab1", "place2", "fR0", "last0", "fin3", "last1", "rows", "ch", "fin2"],
 }
 
 SCRATCH = {
@@ -21,7 +24,7 @@ SCRATCH = {
     "pm": ("sbuf", [128, 128], "float32"),
     "unit": ("sbuf", [128, 1], "float32"),
     "rst": ("sbuf", [128, 256], "float32"),
-    "neg": ("sbuf", [128, 256], "float32"),
+    "neg": ("sbuf", [128, 128], "float32"),
     "eq": ("sbuf", [128, 512], "float8_e4m3fn_x4"),
     "es": ("sbuf", [128, 512], "uint8"),
     "wq": ("sbuf", [128, 3 * Q], "float8_e4m3fn_x4"),
@@ -44,6 +47,8 @@ SCRATCH = {
     "ab": ("sbuf", [128, 5 * IT], "float32"),
     "yt": ("sbuf", [128, 1024], "float32"),
     "nx": ("sbuf", [128, 4], "float32"),
+    "ta": ("sbuf", [32, 96], "float32"),
+    "tb": ("sbuf", [32, 96], "float32"),
     "row": ("sbuf", [1, 64], "float32"),
     "sc0": ("psum", [128, 512], "float32"),
     "sc1": ("psum", [128, 512], "float32"),
@@ -88,9 +93,11 @@ def rank_program(g, core, T, topo):
     def chooser(r):
         return spare(r, True, True)
 
-    def relays(k):
-        return sorted([c for c in range(NCORES) if topo.mates(topo.chip(c), chips[k]) and topo.may_write(c, cores[groups[k][0]])],
-                      key=topo.die)
+    def hand(r):
+        return {"g": spare(r, True, False), "c": chooser(r), "": None}[OPT["via"]]
+
+    relays = [sorted([c for c in range(NCORES) if topo.mates(topo.chip(c), chips[k]) and topo.may_write(c, cores[groups[k][0]])],
+                     key=topo.die) for k in range(ng)]
 
     onward, lands = {}, {}
 
@@ -116,8 +123,8 @@ def rank_program(g, core, T, topo):
                         edge(at, piece, nxt)
                         at = nxt
                     if way[-1] == "b":
-                        rl = relays((k + step[d]) % ng)
-                        nxt = rl[2 * h + j] if halves else rl[2 * j + (part == "R" and OPT.get("sep", False))]
+                        rl = relays[(k + step[d]) % ng]
+                        nxt = rl[2 * h + j] if halves else rl[2 * j + (part == "R" and OPT["sep"])]
                         edge(at, piece, nxt)
                         at = nxt
                     if way[-1] == "a":
@@ -197,37 +204,33 @@ def rank_program(g, core, T, topo):
         s, a, e = piece
         return "a%d" % (4 * (2 * (place[s][0] // 2) + place[s][1]) + a // 128)
 
-    def groups_of(a, pieces):
-        out = {}
-        for p in pieces:
-            if (a, p) in onward:
-                out.setdefault(p[2] - p[1], []).append(p)
-        return list(out.values())
-
-    def arrivals(c):
-        for (a, p), tos in onward.items():
-            if c in tos:
-                side = [q for q in range(len(cores)) if cores[q] == a]
-                share = 1
-                if side and side[0] == p[0]:
-                    part = [q for q in all_pieces(p[0], p[1] // IT) if (a, q) in onward and q[2] - q[1] == p[2] - p[1]
-                            and any((topo.chip(t) == topo.chip(a)) == (topo.chip(c) == topo.chip(a)) for t in onward[(a, q)])]
-                    share = len(part)
-                cnt[piece_sem(p)] = cnt.get(piece_sem(p), 0) + 2 * len(lanes(a, c)) // share
-
     def all_pieces(s, half):
         return sorted(set(p for (a, p) in onward if p[0] == s and p[1] // IT == half), key=lambda p: (p[1] - p[2], p[1]))
 
-    def pass_on(pieces, codes, plane, base):
-        send_mx([(t, codes, plane, base(p) + p[1], base(p) + p[2], T.aq, T["as"], slot(t, p[0]) + p[1], piece_sem(p))
-                 for p in pieces for t in onward[(core, p)]])
+    for (a, p), tos in onward.items():
+        if core in tos:
+            share = 1
+            if a == cores[p[0]]:
+                share = len([q for q in all_pieces(p[0], p[1] // IT) if (a, q) in onward and q[2] - q[1] == p[2] - p[1]
+                             and any((topo.chip(t) == topo.chip(a)) == (topo.chip(core) == topo.chip(a)) for t in onward[(a, q)])])
+            cnt[piece_sem(p)] = cnt.get(piece_sem(p), 0) + 2 * len(lanes(a, core)) // share
+
+    def spread_own(half):
+        out = {}
+        for p in all_pieces(rank, half):
+            if (core, p) in onward:
+                out.setdefault(p[2] - p[1], []).append(p)
+        return [[(t, T.xq, T.xs, p[1], p[2], T.aq, T["as"], slot(t, p[0]) + p[1], piece_sem(p)) for p in ps for t in onward[(core, p)]]
+                for ps in out.values()]
 
     def forward(p):
         wait("g", piece_sem(p))
-        pass_on([p], T.aq, T["as"], lambda q: slot(core, q[0]))
+        a = slot(core, p[0])
+        for tos in ([[t] for t in onward[(core, p)]] if OPT["seq"] else [onward[(core, p)]]):
+            send_mx([(t, T.aq, T["as"], a + p[1], a + p[2], T.aq, T["as"], slot(t, p[0]) + p[1], piece_sem(p)) for t in tos])
 
     v, pe, act, sy = g.vector, g.tensor, g.scalar, g.sync
-    COPY = ActivationFunctionType.Copy
+    COPY, SIGN = ActivationFunctionType.Copy, ActivationFunctionType.Sign
     ADD, MAX, MUL = AluOpType.add, AluOpType.max, AluOpType.mult
     free = {}
 
@@ -250,57 +253,62 @@ def rank_program(g, core, T, topo):
         take(bank)
         return inc(pe.matmul_mx(bank[:, 0:n], codes[:, c0:c0 + 128], plane[:, c0:c0 + 128], T.wq[:, w0:w0 + n], T.ws[:, w0:w0 + n], True, True))
 
-    def over_queries(bank, done, at, n, sem=None):
+    def over_queries(bank, done, at, n):
         wait("v", done)
-        sem = inc(v.tensor_tensor_scan(T.S[:, at:at + n], T.rst[:, 0:n], bank[:, 0:n], 0.0, ADD, MAX), sem)
+        sem = inc(v.tensor_tensor_scan(T.S[:, at:at + n], T.rst[:, 0:n], bank[:, 0:n], 0.0, ADD, MAX))
         free[bank.name] = [sem]
         return sem
 
-    def over_items(b, at, k, halves):
-        take(T.tr)
-        done = None
+    def over_items(b, at, k, halves, banks):
+        p, run = 256 * b, LOW
         for h in range(2):
+            take(banks[h])
             wait("t", *halves[h])
             a = at + 16 * k * h
-            done = inc(pe.transpose(T.tr[0:k, 128 * h:128 * h + 128], T.S[:, a + 15:a + 16 * k:16], T.ident[:, :]), done)
-        p = 256 * b
-        wait("v", done)
-        s2 = inc(v.tensor_tensor_scan(T.P[0:k, p:p + 256], T.tr[0:k, 0:256], T.neg[0:k, :], LOW, MAX, MAX))
-        free["tr"] = [s2]
-        wait("v", s2)
-        lt = inc(v.tensor_scalar(T.lt[0:k, 16 * b:16 * b + 16], T.P[0:k, p + 15:p + 256:16], T.P[0:k, p + 255:p + 256], None, AluOpType.is_lt))
-        wait("v", lt)
-        return inc(v.tensor_reduce(T.cc[0:k, 4 * b:4 * b + 1], T.lt[0:k, 16 * b:16 * b + 16], AxisListType.X, ADD))
+            done = inc(pe.transpose(banks[h][0:k, 0:128], T.S[:, a + 15:a + 16 * k:16], T.ident[:, :]))
+            wait("v", done, *free[banks[0].name])
+            sem = inc(v.tensor_tensor_scan(T.P[0:k, p + 128 * h:p + 128 * h + 128], banks[h][0:k, 0:128], T.neg[0:k, :], run, MAX, MAX))
+            free[banks[h].name] = [sem]
+            run = T.P[0:k, p + 127:p + 128]
+        wait("s", sem)
+        return inc(act.activation(T.lt[0:k, 16 * b:16 * b + 16], T.P[0:k, p + 15:p + 256:16], SIGN,
+                                  bias=T.P[0:k, p + 255:p + 256], scale=-1.0, accum_out=T.cc[0:k, 4 * b:4 * b + 1]))
 
     rank = T.rank_of(core)
-    arrivals(core)
     if rank is None:
-        if core not in lands:
-            return
-        jobs = sorted([p for p in lands[core] if (core, p) in onward], key=lambda p: p[1])
+        handed = [r for r in range(len(cores)) if hand(r) == core]
         mine = [r for r in range(len(cores)) if chooser(r) == core]
+        if core not in lands and not handed:
+            return
+        jobs = sorted([p for p in lands.get(core, []) if (core, p) in onward], key=lambda p: p[1])
+        if mine:
+            ms, kid = constants()
         for p in jobs:
             if p[1] < IT:
                 forward(p)
         if mine:
             s = mine[0]
             far = mate_of(peer_of(s))
-            ms, kid = constants()
             cnt["w1"] = 2 * len(lanes(cores[far], core))
             cnt["w2"] = 2 * len(lanes(cores[s], core))
             wait("t", kid, piece_sem((s, 0, IT)), "w1", "w2")
             wait("v", ms)
+            wait("s", ms)
             halves = []
             for h in range(2):
                 bank = (T.sc0, T.sc1)[h]
                 halves.append([over_queries(bank, scores(bank, T.aq, T["as"], 128 * h, Q, 2 * Q), 256 * h, 256)])
-            wait("g", over_items(0, 0, 16, halves))
+            wait("g", over_items(0, 0, 16, halves, (T.tr, T.ob)))
             col = T.cc[:, 0:1]
             send([(cores[s], col, T.nx[:, 0:1], "n0", 0), (cores[far], col, T.nx[:, 2:3], "n2", 1)])
             send([(cores[mate_of(s)], col, T.nx[:, 3:4], "n3", 0)])
         for p in jobs:
             if p[1] >= IT:
                 forward(p)
+        for r in handed:
+            cnt["c0"] = 2 * OPT["parts"][0] * len(lanes(cores[r], core))
+            wait("g", "c0")
+            send_mx([(cores[peer_of(r)], T.lq, T.ls, 0, 256, T.lq, T.ls, 0, "c0")])
         finish()
         return
 
@@ -309,8 +317,9 @@ def rank_program(g, core, T, topo):
     whole = [groups[(place[rank][0] - step[d]) % ng] for d in range(2)]
     wcols = T.wq[:, 0:Q], T.ws[:, 0:Q]
     n_on, n_off = len(lanes(core, cores[mate])), len(lanes(core, cores[peer]))
-    for name, k in (("w1", 2 * n_off), ("c0", 2 * n_off), ("c1", 2 * n_off), ("c2", 2 * n_on), ("n0", n_on), ("n1", n_off),
-                    ("n2", n_off), ("n3", n_on)):
+    parts = OPT["parts"]
+    for name, k in (("w1", 2 * n_off), ("c0", 2 * n_off * (1 if OPT["via"] else parts[0])), ("c1", 2 * n_off * parts[1]),
+                    ("c2", 2 * n_on * parts[2]), ("n0", n_on), ("n1", n_off), ("n2", n_off), ("n3", n_on)):
         cnt[name] = k
 
     ldq = inc(sy.dma_start(T.qt[:, :], T.qw[:, :]), None, 16)
@@ -321,27 +330,29 @@ def rank_program(g, core, T, topo):
     ms, kid = constants()
     kpm = inc(g.iota(T.pm[:, :], [[0, 8], [1, 16]], 0, 0, allow_small_or_imprecise_dtypes=True))
     inc(v.memset(T.bc[:, :], 0.0), ms)
+    inc(v.memset(T.ta[:, :], 0.0), ms)
     un = inc(v.memset(T.unit[:, :], 1.0 / 64.0))
     wait("v", un)
     inc(v.memset(T.unit[0:8, :], 1.0 / 16.0), ms)
+
+    wait("v", ldq)
+    wqd = inc(v.quantize_mx(wcols[0], wcols[1], T.qt[:, :]))
+    wait("g", wqd)
+    near_q = [(chooser(mate), T.wq, T.ws, 0, Q, T.wq, T.ws, 2 * Q, "w2")]
+    send_mx([(chooser(other), T.wq, T.ws, 0, Q, T.wq, T.ws, Q, "w1")] + near_q * OPT["fuseq"])
+    send_mx([(cores[peer], T.wq, T.ws, 0, Q, T.wq, T.ws, Q, "w1")])
     wait("v", kz)
     eqd = None
     for b in range(4):
         eqd = inc(v.quantize_mx(T.eq[:, 128 * b:128 * b + 128], T.es[:, 128 * b:128 * b + 128], T.zt[:, 3 - b:3 - b + 512]), eqd)
 
-    wait("v", ldq)
-    wqd = inc(v.quantize_mx(wcols[0], wcols[1], T.qt[:, :]))
-    wait("g", wqd)
-    for to in (chooser(other), cores[peer]):
-        send_mx([(to, T.wq, T.ws, 0, Q, T.wq, T.ws, Q, "w1")])
-
     wait("v", ldx)
     xqd = inc(v.quantize_mx(T.xq[:, 0:IT], T.xs[:, 0:IT], T.xr[:, 0:4 * IT]))
     wait("g", xqd)
-    for ps in groups_of(core, all_pieces(rank, 0)):
-        pass_on(ps, T.xq, T.xs, lambda p: 0)
-        if ps[0][2] - ps[0][1] == IT:
-            send_mx([(chooser(mate), T.wq, T.ws, 0, Q, T.wq, T.ws, 2 * Q, "w2")])
+    for n, items in enumerate(spread_own(0)):
+        send_mx(items)
+        if n == 0 and not OPT["fuseq"]:
+            send_mx(near_q)
     wait("t", xqd, eqd)
     ybank = [T.y0, T.y1, T.y2, T.y3]
     dm = [inc(pe.matmul_mx(ybank[b][:, 0:IT], T.eq[:, 128 * b:128 * b + 128], T.es[:, 128 * b:128 * b + 128],
@@ -354,28 +365,27 @@ def rank_program(g, core, T, topo):
     wait("v", rs)
     rq = inc(v.quantize_mx(T.xq[:, IT:2 * IT], T.xs[:, IT:2 * IT], T.xr[:, 4 * IT:8 * IT]))
     wait("g", rq)
-    for ps in groups_of(core, all_pieces(rank, 1)):
-        pass_on(ps, T.xq, T.xs, lambda p: 0)
+    for items in spread_own(1):
+        send_mx(items)
 
     def landed(q, s, half):
         wait(q, *[piece_sem(p) for p in lands[core] if p[0] == s and p[1] // IT == half])
 
-    def both(bank, codes, plane, c0, n, l):
+    def both(bank, codes, plane, c0, n, out):
         take(bank)
         pe.matmul_mx(bank[:, 0:n], wcols[0], wcols[1], codes[:, c0:c0 + n], plane[:, c0:c0 + n], True, False)
         done = inc(pe.matmul_mx(bank[:, 0:n], wcols[0], wcols[1], codes[:, c0 + n:c0 + 2 * n], plane[:, c0 + n:c0 + 2 * n], False, True))
         wait("s", done)
-        out = inc(act.activation(l, bank[:, 0:n], COPY))
-        free[bank.name] = [out]
-        return out
+        sem = inc(act.activation(out, bank[:, 0:n], COPY))
+        free[bank.name] = [sem]
+        return sem
 
     def spread(b, col, k, done, unit):
         wait("v", done, kpm)
         bcd = inc(v.tensor_scalar(T.bc[0:k, 128 * b:128 * b + 128], T.pm[0:k, :], unit, col, MUL, ADD))
         take(T.ob)
         wait("t", bcd)
-        obd = inc(pe.transpose(T.ob[:, 128 * b:128 * b + 128], T.bc[:, 128 * b:128 * b + 128], T.ident[:, :]))
-        wait("v", obd)
+        return inc(pe.transpose(T.ob[:, 128 * b:128 * b + 128], T.bc[:, 128 * b:128 * b + 128], T.ident[:, :]))
 
     def lists(f, c0, k):
         sem = None
@@ -384,62 +394,80 @@ def rank_program(g, core, T, topo):
         free["ob"] = free.get("ob", []) + [sem]
         return sem
 
-    def tile(i, f, ofd, to):
-        a, vx = 1024 * i, OPT["vx"]
-        wait("s", ofd, rs)
-        gr = inc(act.activation(T.gt[:, a + 512:a + 1024], T.xr[:, 1024:2048].indirect(T.of[:, f:f + 32]), COPY))
-        if vx < 512:
-            inc(act.activation(T.gt[:, a + vx:a + 512], T.xr[:, 0:1024].indirect(T.of[:, f + vx // 16:f + 32]), COPY), gr)
-        wait("v", ofd)
-        gx = inc(v.tensor_copy(T.gt[:, a:a + vx], T.xr[:, 0:1024].indirect(T.of[:, f:f + vx // 16])))
-        wait("v", gx, gr)
-        qz = inc(v.quantize_mx(T.cq[:, 256 * i:256 * i + 256], T.cs[:, 256 * i:256 * i + 256], T.gt[:, a:a + 1024]))
-        wait("g", qz)
-        send_mx([(cores[to], T.cq, T.cs, 256 * i, 256 * i + 256, T.lq, T.ls, 256 * i, "c%d" % i)])
+    def pick_from(q, out, win, offs):
+        win = win.indirect(offs)
+        return inc(v.tensor_copy(out, win) if q == "v" else act.activation(out, win, COPY))
 
-    stores = []
+    def gather(i, f, ofd):
+        a, vx = 1024 * i, OPT["vx"][i]
+        wait("s", ofd, rs)
+        wait("v", ofd)
+        cuts = [("s", 512, 1024), ("s", vx, 512), ("v", 0, vx)] if parts[i] == 1 else \
+            [("v", 0, 256), ("s", 256, 512), ("s", 512 + vx // 2, 1024), ("v", 512, 512 + vx // 2)]
+        st["g", i] = []
+        for q, b, e in cuts:
+            if b < e:
+                w = 1024 * (b // 512)
+                st["g", i].append((b, pick_from(q, T.gt[:, a + b:a + e], T.xr[:, w:w + 1024], T.of[:, f + b % 512 // 16:f + (e - 1) % 512 // 16 + 1])))
+            if parts[i] == 2 and e == 512:
+                pack(i, 0, 128)
+
+    def pack(i, b, e):
+        to = hand(rank) if i == 0 and OPT["via"] else cores[(peer, other, mate)[i]]
+        c = 256 * i
+        wait("v", *[sem for at, sem in st["g", i] if 4 * b <= at < 4 * e])
+        qz = inc(v.quantize_mx(T.cq[:, c + b:c + e], T.cs[:, c + b:c + e], T.gt[:, 4 * (c + b):4 * (c + e)]))
+        wait("g", qz)
+        send_mx([(to, T.cq, T.cs, c + b, c + e, T.lq, T.ls, c + b, "c%d" % i)])
 
     def store(s, n, done):
-        wait("y", *done)
-        stores.append(inc(sy.dma_start(T.y[:, 128 * s:128 * (s + n)], T.yt[:, 128 * s:128 * (s + n)]), None, 16))
+        wait("y", done)
+        inc(sy.dma_start(T.y[:, 128 * s:128 * (s + n)], T.yt[:, 128 * s:128 * (s + n)]), None, 16)
 
     wait("t", wqd, kid)
     wait("v", ms)
+    wait("s", ms)
     halves = [[over_queries((T.sc0, T.sc1)[h], scores((T.sc0, T.sc1)[h], T.xq, T.xs, 128 * h, 0, Q), 256 * h, Q)] for h in range(2)]
     wait("t", rq)
-    st = {"ab": [both(T.y2, T.xq, T.xs, 0, IT, T.ab[:, 0:IT])], "near": [[], []]}
+    st = {("ab", 0): both(T.y2, T.xq, T.xs, 0, IT, T.ab[:, 0:IT]), "near": [[], []], "row": None}
     wait("t", "w1")
     for h in range(2):
         halves[h].append(over_queries(ybank[h], scores(ybank[h], T.xq, T.xs, 128 * h, Q, Q), 256 * h + Q, Q))
-    first = over_items(0, 0, 16, halves)
-    spread(0, T.cc[0:16, 0:1], 16, first, T.unit[0:16, :])
+    first = over_items(0, 0, 16, halves, (T.tr, T.y3))
+    wait("v", spread(0, T.cc[0:16, 0:1], 16, first, T.unit[0:16, :]))
     of1 = lists(0, 8, 8)
     of0 = inc(v.tensor_scalar(T.of[:, 32:40], T.ob[:, 0:8], 16.0, None, MUL))
     free["ob"].append(of0)
 
-    def t1():
-        tile(0, 0, of1, peer)
+    def tell():
         wait("g", first)
         send([(cores[peer], T.cc[:, 0:1], T.nx[:, 1:2], "n1", 0)])
-        wait("v", of0, st["ab"][0])
-        store(rank, 1, [inc(v.tensor_copy(T.yt[:, 128 * rank:128 * rank + 128], T.ab[:, 0:IT].indirect(T.of[:, 32:40])))])
+
+    def own():
+        wait(OPT["own"], of0, st["ab", 0])
+        store(rank, 1, pick_from(OPT["own"], T.yt[:, 128 * rank:128 * rank + 128], T.ab[:, 0:IT], T.of[:, 32:40]))
 
     def near(d):
         banks = ((T.sc0, T.sc1, T.y2, T.y3), (T.y0, T.y1, T.sc0, T.sc1))[d]
-        for j, s in enumerate(whole[d]):
+        j0 = place[rank][1]
+        for n, j in enumerate((j0, 1 - j0)):
+            s = whole[d][j]
             landed("t", s, 0)
             for h in range(2):
-                bank = banks[2 * j + h]
+                bank = banks[2 * n + h]
                 done = scores(bank, T.aq, T["as"], slot(core, s) + 128 * h, 0, Q)
                 st["near"][h].append(over_queries(bank, done, 512 + 512 * h + 128 * (2 * d + j), Q))
 
-    def fwd():
+    def fwd(i, d):
         for p in lands[core]:
-            if (core, p) in onward:
+            if (core, p) in onward and p[1] // IT == i and p[0] in whole[d]:
                 forward(p)
 
     def num():
-        spread(1, T.nx[0:16, 0:1], 16, "n0", 1.0 / 64.0)
+        st["num"] = spread(1, T.nx[0:16, 0:1], 16, "n0", 1.0 / 64.0)
+
+    def num2():
+        wait("v", st["num"])
         st["of"] = lists(64, 128, 16)
 
     def ab(d):
@@ -447,53 +475,61 @@ def rank_program(g, core, T, topo):
             landed("t", s, 0)
             landed("t", s, 1)
             l = 1 + 2 * d + j
-            st["ab"].append(both(((T.y2, T.y3), (T.y0, T.y1))[d][j], T.aq, T["as"], slot(core, s), IT, T.ab[:, IT * l:IT * l + IT]))
+            st["ab", l] = both(((T.y2, T.y3), (T.y0, T.y1))[d][j], T.aq, T["as"], slot(core, s), IT, T.ab[:, IT * l:IT * l + IT])
 
     def fin(i):
         s = (peer, other, mate)[i]
         wait("t", "c%d" % i)
-        store(s, 1, [both((T.sc0, T.sc1, T.sc0)[i], T.lq, T.ls, 256 * i, 128, T.yt[:, 128 * s:128 * s + 128])])
+        store(s, 1, both((T.sc0, T.sc1, T.sc0)[i], T.lq, T.ls, 256 * i, 128, T.yt[:, 128 * s:128 * s + 128]))
 
     def pick():
-        done = over_items(1, 512, 32, st["near"])
-        spread(2, T.cc[0:32, 4:5], 32, done, 1.0 / 16.0)
+        assert len(st["near"][0]) == 4
+        st["pick"] = over_items(1, 512, 32, st["near"], (T.tr, T.sc1))
+
+    def place1():
+        assert "of" in st
+        st["place"] = spread(2, T.cc[0:32, 4:5], 32, st["pick"], 1.0 / 16.0)
+
+    def place2():
+        wait("v", st["place"])
         sem = None
         for l in range(4):
             sem = inc(v.tensor_scalar(T.of[:, 128 + 8 * l:136 + 8 * l], T.ob[:, 256 + 8 * l:264 + 8 * l], 16.0, float(IT * (l % 2)), MUL, ADD), sem)
         st["ofn"] = sem
-        free["ob"].append(sem)
-        src = {rank: T.ob[0:1, 0:8], peer: T.ob[0:1, 392:400], other: T.tr[0:1, 256:264], mate: T.tr[0:1, 392:400]}
-        for l, s in enumerate(whole[0] + whole[1]):
-            src[s] = T.ob[0:1, 256 + 8 * l:264 + 8 * l]
-        st["src"] = src
+
+    def into_row(src):
+        sem = None
+        for s in src:
+            sem = inc(v.tensor_copy(T.row[0:1, s:64:8], src[s]), sem)
+        return sem
 
     def rows():
-        sem = None
-        take(T.tr)
-        take(T.ob)
-        for n, out in ((1, T.ob[0:1, 384:512]), (2, T.tr[0:1, 256:384]), (3, T.tr[0:1, 384:512])):
-            wait("t", "n%d" % n)
-            sem = inc(pe.transpose(out, T.nx[:, n:n + 1], T.ident[:, :]), sem)
-        st["rows"] = sem
+        wait("v", "n1", "n2", "n3")
+        wait("v", inc(v.tensor_copy(T.ta[:, 0:96:32], T.nx[0:32, 1:4])))
+        wait("v", inc(v.transpose(T.tb[:, :], T.ta[:, :])))
+        st["row"] = into_row({peer: T.tb[0:1, 8:16], other: T.tb[0:1, 32:40], mate: T.tb[0:1, 72:80]})
 
-    def last():
-        for d in range(2):
-            q = "vs"[d]
-            s = whole[d][0]
-            wait(q, st["ofn"], st["ab"][1 + 2 * d], st["ab"][2 + 2 * d])
-            out, win = T.yt[:, 128 * s:128 * s + 256], T.ab[:, IT * (1 + 2 * d):IT * (3 + 2 * d)].indirect(T.of[:, 128 + 16 * d:144 + 16 * d])
-            store(s, 2, [inc(v.tensor_copy(out, win) if q == "v" else act.activation(out, win, COPY))])
-        sem = None
-        wait("v", st["rows"])
-        for s in range(NR):
-            sem = inc(v.tensor_copy(T.row[0:1, s:64:8], st["src"][s]), sem)
-        wait("s", sem)
+    def last(d):
+        q = "vs"[d]
+        s = whole[d][0]
+        wait(q, st["ofn"], st["ab", 1 + 2 * d], st["ab", 2 + 2 * d])
+        store(s, 2, pick_from(q, T.yt[:, 128 * s:128 * s + 256], T.ab[:, IT * (1 + 2 * d):IT * (3 + 2 * d)], T.of[:, 128 + 16 * d:144 + 16 * d]))
+
+    def numbers():
+        assert st["row"] and "ofn" in st
+        src = {s: T.ob[0:1, 256 + 8 * l:264 + 8 * l] for l, s in enumerate(whole[0] + whole[1])}
+        src[rank] = T.ob[0:1, 0:8]
+        wait("s", st["row"], into_row(src))
         inc(act.dma_start(T.ch[:, :], T.row[0:1, :]), None, 16)
 
-    steps = {"t1": t1, "near0": lambda: near(0), "near1": lambda: near(1), "fwd": fwd, "num": num,
-             "t2": lambda: tile(1, 64, st["of"], other), "t3": lambda: tile(2, 96, st["of"], mate),
+    steps = {"g1": lambda: gather(0, 0, of1), "g2": lambda: gather(1, 64, st["of"]), "g3": lambda: gather(2, 96, st["of"]),
+             "p1": lambda: pack(0, 128 * (parts[0] - 1), 256), "p2": lambda: pack(1, 128 * (parts[1] - 1), 256),
+             "p3": lambda: pack(2, 128 * (parts[2] - 1), 256), "own": own, "tell": tell,
+             "near0": lambda: near(0), "near1": lambda: near(1), "num": num, "num2": num2,
+             "fx0": lambda: fwd(0, 0), "fx1": lambda: fwd(0, 1), "fR0": lambda: fwd(1, 0), "fR1": lambda: fwd(1, 1),
              "ab0": lambda: ab(0), "ab1": lambda: ab(1), "fin1": lambda: fin(0), "fin2": lambda: fin(1), "fin3": lambda: fin(2),
-             "pick": pick, "rows": rows, "last": last}
+             "pick": pick, "place": place1, "place2": place2, "rows": rows, "last0": lambda: last(0), "last1": lambda: last(1),
+             "ch": numbers}
     for name in OPT["order"]:
         steps[name]()
     finish()

@@ -5,13 +5,14 @@ NR, Q, IT = 8, 128, 256
 LOW = -5.0e29
 NCORES = 128
 OPT = {
-    "route": {("x", 0): "r", ("R", 0): "c", ("x", 1): "cr", ("R", 1): "b"},
-    "split": True, "sep": False, "seq": True, "via": "", "fuseq": 0,
-    "vx": [512, 512, 448],
-    "parts": [1, 1, 1],
-    "own": "s",
-    "order": ["fx0", "fx1", "num", "g1", "num2", "p1", "g2", "tell", "p2", "g3", "own", "p3", "near0", "near1", "pick", "fR1",
-              "ab0", "fin1", "place", "ab1", "place2", "fR0", "last0", "fin3", "last1", "rows", "ch", "fin2"],
+    "route": {("x", 0): "a", ("R", 0): "b", ("x", 1): "ca", ("R", 1): "ca"},
+    "split": False, "via": -1, "off": True, "late": 0, "jq": 1, "hr": 0, "qm": 2,
+    "lane": {"x0": "A", "R0": "B", "R1": "B"},
+    "jo": ["x0", "x1", "n", "R1"], "js": [(0, 0), (0, 1), (1, 0), (1, 1)],
+    "vx": [512, 512, 512],
+    "own": "s", "cp": list("sssvvsvvs"),
+    "order": ["g1", "own", "tell", "p1", "num", "num2", "num3", "g2", "num4", "p2", "g3", "p3", "fin1", "a00", "place", "rows",
+              "place2", "a01", "ch", "a10", "last0", "a11", "fin3", "last1", "fin2"],
 }
 
 SCRATCH = {
@@ -22,6 +23,7 @@ SCRATCH = {
     "zt": ("sbuf", [128, 516], "bfloat16"),
     "ident": ("sbuf", [128, 128], "float32"),
     "pm": ("sbuf", [128, 128], "float32"),
+    "p16": ("sbuf", [128, 128], "float32"),
     "unit": ("sbuf", [128, 1], "float32"),
     "rst": ("sbuf", [128, 256], "float32"),
     "neg": ("sbuf", [128, 128], "float32"),
@@ -33,11 +35,11 @@ SCRATCH = {
     "xs": ("sbuf", [128, 2 * IT], "uint8"),
     "aq": ("sbuf", [128, 8 * IT], "float8_e4m3fn_x4"),
     "as": ("sbuf", [128, 8 * IT], "uint8"),
-    "S": ("sbuf", [128, 1536], "float32"),
+    "S": ("sbuf", [128, 2048], "float32"),
     "P": ("sbuf", [128, 512], "float32"),
     "lt": ("sbuf", [128, 32], "float32"),
     "cc": ("sbuf", [128, 8], "float32"),
-    "bc": ("sbuf", [128, 384], "float32"),
+    "bc": ("sbuf", [128, 512], "float32"),
     "of": ("sbuf", [128, 192], "uint16"),
     "gt": ("sbuf", [128, 3 * 1024], "bfloat16"),
     "cq": ("sbuf", [128, 3 * 256], "float8_e4m3fn_x4"),
@@ -46,7 +48,7 @@ SCRATCH = {
     "ls": ("sbuf", [128, 3 * 256], "uint8"),
     "ab": ("sbuf", [128, 5 * IT], "float32"),
     "yt": ("sbuf", [128, 1024], "float32"),
-    "nx": ("sbuf", [128, 4], "float32"),
+    "nx": ("sbuf", [128, 8], "float32"),
     "ta": ("sbuf", [32, 96], "float32"),
     "tb": ("sbuf", [32, 96], "float32"),
     "row": ("sbuf", [1, 64], "float32"),
@@ -60,7 +62,7 @@ SCRATCH = {
     "y3": ("psum", [128, 512], "float32"),
 }
 SEMAPHORES = (["lsem", "w1", "w2"] + ["a%d" % i for i in range(16)] + ["c%d" % i for i in range(3)]
-              + ["n%d" % i for i in range(4)] + ["u%d" % i for i in range(120)])
+              + ["n%d" % i for i in range(7)] + ["u%d" % i for i in range(120)])
 
 
 def rank_program(g, core, T, topo):
@@ -90,12 +92,9 @@ def rank_program(g, core, T, topo):
         return [c for c in topo.cores_of(own) if T.rank_of(c) is None and (topo.die(c) != topo.die(own)) == other_die
                 and all(topo.may_write(c, t) for t in cores) == free][place[r][1]]
 
-    def chooser(r):
-        return spare(r, True, True)
-
-    def hand(r):
-        return {"g": spare(r, True, False), "c": chooser(r), "": None}[OPT["via"]]
-
+    chooser = [spare(r, True, True) for r in range(len(cores))]
+    judge = [spare(r, False, False) for r in range(len(cores))]
+    idle = [spare(r, True, False) for r in range(len(cores))]
     relays = [sorted([c for c in range(NCORES) if topo.mates(topo.chip(c), chips[k]) and topo.may_write(c, cores[groups[k][0]])],
                      key=topo.die) for k in range(ng)]
 
@@ -110,33 +109,21 @@ def rank_program(g, core, T, topo):
         for s in range(len(cores)):
             k, j = place[s]
             if part == "x":
-                edge(cores[s], (s, 0, IT), chooser(s))
+                edge(cores[s], (s, 0, IT), chooser[s])
             for d in range(2):
                 to = groups[(k + step[d]) % ng]
                 way = OPT["route"][(part, d)]
                 halves = OPT["split"] and way == "b"
                 for h in range(2 if halves else 1):
                     piece = (s, c0 + 128 * h, c0 + 128 * h + 128) if halves else (s, c0, c0 + IT)
-                    at = cores[s]
-                    if way[0] in "cg":
-                        nxt = chooser(s) if way[0] == "c" else spare(s, True, False)
-                        edge(at, piece, nxt)
-                        at = nxt
-                    if way[-1] == "b":
-                        rl = relays[(k + step[d]) % ng]
-                        nxt = rl[2 * h + j] if halves else rl[2 * j + (part == "R" and OPT["sep"])]
-                        edge(at, piece, nxt)
-                        at = nxt
-                    if way[-1] == "a":
-                        nxt = spare(to[j], False, False)
-                        edge(at, piece, nxt)
-                        at = nxt
-                    if way[-1] == "r":
-                        edge(at, piece, cores[to[j]])
-                        edge(cores[to[j]], piece, cores[to[1 - j]])
-                    else:
-                        for t in (to[j], to[1 - j]):
-                            edge(at, piece, cores[t])
+                    rl = relays[(k + step[d]) % ng]
+                    at = {"c": chooser[s], "b": rl[2 * h + j] if halves else rl[2 * j + d], "a": judge[to[j]], "i": idle[to[j]],
+                          "r": cores[to[j]]}
+                    stops = [cores[s]] + [at[w] for w in way]
+                    for a, b in zip(stops, stops[1:]):
+                        edge(a, piece, b)
+                    for t in (to[j], to[1 - j])[way[-1] == "r":]:
+                        edge(stops[-1], piece, cores[t])
 
     def slot(c, s):
         r = T.rank_of(c)
@@ -168,25 +155,32 @@ def rank_program(g, core, T, topo):
             if top.get(name, 0) < cnt[name]:
                 wait("g", name)
 
-    def lanes(a, b):
-        far = [c for c in cores if topo.chip(c) != topo.chip(a) and topo.may_write(a, c)][0]
+    def lanes(a, b, what=None):
+        eng = topo.engines(a, b)
         if topo.chip(a) != topo.chip(b):
-            return topo.engines(a, b)
-        return [e for e in topo.engines(a, b) if e not in topo.engines(a, far)]
+            w = OPT["lane"].get(what, "8") if a in cores else "8"
+            return eng if w == "8" else eng[:len(eng) // 2] if w == "A" else eng[len(eng) // 2:]
+        if a in judge or a in idle:
+            return eng
+        far = [c for c in cores if topo.chip(c) != topo.chip(a) and topo.may_write(a, c)][0]
+        return [e for e in eng if e not in topo.engines(a, far)]
+
+    def kind_of(p, b):
+        d = [d for d in range(2) if b in relays[(place[p[0]][0] + step[d]) % ng] or topo.chip(b) == chips[(place[p[0]][0] + step[d]) % ng]]
+        return "xR"[p[1] // IT] + str(d[0]) if d else None
 
     def send(items):
         kinds = {}
         for it in items:
-            kinds.setdefault(topo.chip(it[0]) == topo.chip(core), {}).setdefault(it[4], []).append(it)
+            kinds.setdefault(tuple(lanes(core, it[0], *it[5:])), {}).setdefault(it[4], []).append(it)
         moves = []
-        for kind in kinds.values():
+        for all_eng, kind in kinds.items():
             for n, its in enumerate(kind.values()):
-                eng = lanes(core, its[0][0])
-                eng = eng[n * len(eng) // len(kind):(n + 1) * len(eng) // len(kind)]
+                eng = all_eng[n * len(all_eng) // len(kind):(n + 1) * len(all_eng) // len(kind)]
                 moves.append((its, sum(1 << e for e in eng)))
                 cnt["lsem"] = cnt.get("lsem", 0) + len(eng)
         if len(items) == 1:
-            to, src, dst, sem, _ = items[0]
+            to, src, dst, sem = items[0][:4]
             rid, pid, _ = topo.addr(to)
             g.remote_dma(out_ap=dst, in_ap=src, remote_sem=T.sem[sem], local_sem=T.sem["lsem"], pid=pid,
                          routing_id=rid, dma_engine_mask=moves[0][1])
@@ -196,9 +190,9 @@ def rank_program(g, core, T, topo):
                                               dsts=[it[2] for it in its]) for its, m in moves], local_sem=T.sem["lsem"])
 
     def send_mx(items):
-        send([(i[0], i[1][:, i[3]:i[4]].bitcast(dt.uint8), i[5][:, i[7]:i[7] + i[4] - i[3]].bitcast(dt.uint8), i[8], (i[3], i[8]))
+        send([(i[0], i[1][:, i[3]:i[4]].bitcast(dt.uint8), i[5][:, i[7]:i[7] + i[4] - i[3]].bitcast(dt.uint8), i[8], (i[3], i[8])) + i[9:]
               for i in items])
-        send([(i[0], i[2][:, i[3]:i[4]], i[6][:, i[7]:i[7] + i[4] - i[3]], i[8], (i[3], i[8])) for i in items])
+        send([(i[0], i[2][:, i[3]:i[4]], i[6][:, i[7]:i[7] + i[4] - i[3]], i[8], (i[3], i[8])) + i[9:] for i in items])
 
     def piece_sem(piece):
         s, a, e = piece
@@ -209,25 +203,28 @@ def rank_program(g, core, T, topo):
 
     for (a, p), tos in onward.items():
         if core in tos:
-            share = 1
-            if a == cores[p[0]]:
-                share = len([q for q in all_pieces(p[0], p[1] // IT) if (a, q) in onward and q[2] - q[1] == p[2] - p[1]
-                             and any((topo.chip(t) == topo.chip(a)) == (topo.chip(core) == topo.chip(a)) for t in onward[(a, q)])])
-            cnt[piece_sem(p)] = cnt.get(piece_sem(p), 0) + 2 * len(lanes(a, core)) // share
+            share = 2 if a == cores[p[0]] and p[2] - p[1] < IT else 1
+            cnt[piece_sem(p)] = cnt.get(piece_sem(p), 0) + 2 * len(lanes(a, core, kind_of(p, core) if a == cores[p[0]] else None)) // share
 
-    def spread_own(half):
-        out = {}
+    def own_codes(half):
+        calls = []
         for p in all_pieces(rank, half):
-            if (core, p) in onward:
-                out.setdefault(p[2] - p[1], []).append(p)
-        return [[(t, T.xq, T.xs, p[1], p[2], T.aq, T["as"], slot(t, p[0]) + p[1], piece_sem(p)) for p in ps for t in onward[(core, p)]]
-                for ps in out.values()]
+            for t in onward.get((core, p), []):
+                it = (t, T.xq, T.xs, p[1], p[2], T.aq, T["as"], slot(t, p[0]) + p[1], piece_sem(p), kind_of(p, t))
+                mine = set(lanes(core, t, it[9]))
+                fit = [c for c in calls if c[0][4] - c[0][3] == p[2] - p[1]
+                       and all(mine.isdisjoint(lanes(core, o[0], o[9])) or (o[9] == it[9] and o[3] != it[3]) for o in c)]
+                if fit:
+                    fit[0].append(it)
+                else:
+                    calls.append([it])
+        return calls
 
     def forward(p):
         wait("g", piece_sem(p))
         a = slot(core, p[0])
-        for tos in ([[t] for t in onward[(core, p)]] if OPT["seq"] else [onward[(core, p)]]):
-            send_mx([(t, T.aq, T["as"], a + p[1], a + p[2], T.aq, T["as"], slot(t, p[0]) + p[1], piece_sem(p)) for t in tos])
+        for t in onward[(core, p)]:
+            send_mx([(t, T.aq, T["as"], a + p[1], a + p[2], T.aq, T["as"], slot(t, p[0]) + p[1], piece_sem(p))])
 
     v, pe, act, sy = g.vector, g.tensor, g.scalar, g.sync
     COPY, SIGN = ActivationFunctionType.Copy, ActivationFunctionType.Sign
@@ -249,66 +246,101 @@ def rank_program(g, core, T, topo):
         kid = inc(g.affine_select(T.ident[:, :], T.onf[:, :], [[-1, 128]], AluOpType.is_equal, 0.0, 0, 1))
         return ms, kid
 
-    def scores(bank, codes, plane, c0, w0, n):
+    def over_queries(bank, codes, plane, c0, w0, n, at):
         take(bank)
-        return inc(pe.matmul_mx(bank[:, 0:n], codes[:, c0:c0 + 128], plane[:, c0:c0 + 128], T.wq[:, w0:w0 + n], T.ws[:, w0:w0 + n], True, True))
-
-    def over_queries(bank, done, at, n):
-        wait("v", done)
+        wait("v", inc(pe.matmul_mx(bank[:, 0:n], codes[:, c0:c0 + 128], plane[:, c0:c0 + 128], T.wq[:, w0:w0 + n], T.ws[:, w0:w0 + n], True, True)))
         sem = inc(v.tensor_tensor_scan(T.S[:, at:at + n], T.rst[:, 0:n], bank[:, 0:n], 0.0, ADD, MAX))
         free[bank.name] = [sem]
         return sem
 
-    def over_items(b, at, k, halves, banks):
-        p, run = 256 * b, LOW
+    def over_items(k, halves, banks, at=0, b=0):
+        run, p = LOW, 256 * b
         for h in range(2):
             take(banks[h])
             wait("t", *halves[h])
-            a = at + 16 * k * h
-            done = inc(pe.transpose(banks[h][0:k, 0:128], T.S[:, a + 15:a + 16 * k:16], T.ident[:, :]))
+            done = inc(pe.transpose(banks[h][0:k, 0:128], T.S[:, at + 16 * k * h + 15:at + 16 * k * (h + 1):16], T.ident[:, :]))
             wait("v", done, *free[banks[0].name])
             sem = inc(v.tensor_tensor_scan(T.P[0:k, p + 128 * h:p + 128 * h + 128], banks[h][0:k, 0:128], T.neg[0:k, :], run, MAX, MAX))
             free[banks[h].name] = [sem]
             run = T.P[0:k, p + 127:p + 128]
         wait("s", sem)
-        return inc(act.activation(T.lt[0:k, 16 * b:16 * b + 16], T.P[0:k, p + 15:p + 256:16], SIGN,
-                                  bias=T.P[0:k, p + 255:p + 256], scale=-1.0, accum_out=T.cc[0:k, 4 * b:4 * b + 1]))
+        return inc(act.activation(T.lt[0:k, 16 * b:16 * b + 16], T.P[0:k, p + 15:p + 256:16], SIGN, bias=T.P[0:k, p + 255:p + 256],
+                                  scale=-1.0, accum_out=T.cc[0:k, 4 * b:4 * b + 1]))
 
     rank = T.rank_of(core)
+    ybank = [T.y0, T.y1, T.y2, T.y3]
     if rank is None:
-        handed = [r for r in range(len(cores)) if hand(r) == core]
-        mine = [r for r in range(len(cores)) if chooser(r) == core]
-        if core not in lands and not handed:
+        if core not in lands:
             return
-        jobs = sorted([p for p in lands.get(core, []) if (core, p) in onward], key=lambda p: p[1])
-        if mine:
+        col = T.cc[:, 0:1]
+        jobs = sorted([p for p in lands[core] if (core, p) in onward], key=lambda p: p[1])
+        judging = core in judge and OPT["off"]
+        if core in chooser or judging:
             ms, kid = constants()
-        for p in jobs:
-            if p[1] < IT:
-                forward(p)
-        if mine:
-            s = mine[0]
+            wait("t", kid)
+            wait("v", ms)
+            wait("s", ms)
+        tell = []
+        if core in chooser:
+            s = chooser.index(core)
             far = mate_of(peer_of(s))
             cnt["w1"] = 2 * len(lanes(cores[far], core))
             cnt["w2"] = 2 * len(lanes(cores[s], core))
-            wait("t", kid, piece_sem((s, 0, IT)), "w1", "w2")
-            wait("v", ms)
-            wait("s", ms)
-            halves = []
-            for h in range(2):
-                bank = (T.sc0, T.sc1)[h]
-                halves.append([over_queries(bank, scores(bank, T.aq, T["as"], 128 * h, Q, 2 * Q), 256 * h, 256)])
-            wait("g", over_items(0, 0, 16, halves, (T.tr, T.ob)))
-            col = T.cc[:, 0:1]
-            send([(cores[s], col, T.nx[:, 0:1], "n0", 0), (cores[far], col, T.nx[:, 2:3], "n2", 1)])
-            send([(cores[mate_of(s)], col, T.nx[:, 3:4], "n3", 0)])
+            wait("t", piece_sem((s, 0, IT)), "w1")
+            one = over_items(8, [[over_queries(ybank[h], T.aq, T["as"], 128 * h, Q, Q, 128 * h)] for h in range(2)], (T.tr, T.ob))
+            wait("t", "w2")
+            two = over_items(8, [[over_queries(ybank[2 + h], T.aq, T["as"], 128 * h, 2 * Q, Q, 256 + 128 * h)] for h in range(2)],
+                             (T.tr, T.ob), 256, 1)
+            tell = [(one, [(cores[s], col, T.nx[:, 0:1], "n0", 0), (cores[far], col, T.nx[:, 2:3], "n2", 1)]),
+                    (two, [(cores[s], T.cc[:, 4:5], T.nx[:, 6:7], "n6", 0)]),
+                    (two, [(cores[mate_of(s)], T.cc[:, 4:5], T.nx[:, 3:4], "n3", 0)])]
+        if judging:
+            k, j = place[judge.index(core)]
+            wait("v", inc(v.memset(T.S[:, 15:2048:16], 0.0)))
+            if OPT["jq"]:
+                twin = judge[groups[k][1 - j]]
+                cnt["w1"], cnt["w2"] = 2 * len(lanes(cores[groups[k][j]], core)), 2 * len(lanes(twin, core))
+                wait("g", "w1")
+                send_mx([(twin, T.wq, T.ws, Q + Q * j, 2 * Q + Q * j, T.wq, T.ws, Q + Q * j, "w2")])
+                wait("t", "w1")
+            else:
+                cnt["w2"] = sum(2 * len(lanes(cores[r], core)) for r in groups[k])
+                wait("t", "w2")
+            halves = [[], []]
+            six = ybank + [T.sc0, T.sc1]
+            for n, (d, far) in enumerate(OPT["js"]):
+                s = groups[(k - step[d]) % ng][j]
+                i = (j + far) % 2
+                wait("t", piece_sem((s, 0, IT)), *["w2"] * far)
+                for h in range(2):
+                    halves[h].append(over_queries(six[(2 * n + h) % 6], T.aq, T["as"], slot(core, s) + 128 * h, Q + Q * i, Q,
+                                                  1024 * h + 256 * (2 * j + d) + 128 * i))
+            chosen = over_items(64, halves, (T.tr, T.ob))
+            for what in OPT["jo"]:
+                if what == "n":
+                    wait("g", chosen)
+                    send([(cores[r], col, T.nx[:, 4 + j:5 + j], "n%d" % (4 + j), 0) for r in groups[k]])
+                for p in jobs:
+                    if what == "xR"[p[1] // IT] + str([(k - step[d]) % ng for d in range(2)].index(place[p[0]][0])):
+                        forward(p)
+            jobs = []
         for p in jobs:
-            if p[1] >= IT:
+            if p[1] < IT:
                 forward(p)
-        for r in handed:
-            cnt["c0"] = 2 * OPT["parts"][0] * len(lanes(cores[r], core))
-            wait("g", "c0")
-            send_mx([(cores[peer_of(r)], T.lq, T.ls, 0, 256, T.lq, T.ls, 0, "c0")])
+        for n, (done, items) in enumerate(tell):
+            wait("g", done)
+            send(items)
+            for p in jobs:
+                if p[1] >= IT and n == OPT["hr"]:
+                    forward(p)
+        for p in jobs:
+            if p[1] >= IT and not tell:
+                forward(p)
+        if core in chooser and OPT["via"] >= 0:
+            i, s = OPT["via"], chooser.index(core)
+            cnt["c%d" % i] = 2 * len(lanes(cores[s], core))
+            wait("g", "c%d" % i)
+            send_mx([(cores[(peer_of(s), mate_of(peer_of(s)))[i]], T.lq, T.ls, 256 * i, 256 * i + 256, T.lq, T.ls, 256 * i, "c%d" % i)])
         finish()
         return
 
@@ -316,10 +348,9 @@ def rank_program(g, core, T, topo):
     other = mate_of(peer)
     whole = [groups[(place[rank][0] - step[d]) % ng] for d in range(2)]
     wcols = T.wq[:, 0:Q], T.ws[:, 0:Q]
-    n_on, n_off = len(lanes(core, cores[mate])), len(lanes(core, cores[peer]))
-    parts = OPT["parts"]
-    for name, k in (("w1", 2 * n_off), ("c0", 2 * n_off * (1 if OPT["via"] else parts[0])), ("c1", 2 * n_off * parts[1]),
-                    ("c2", 2 * n_on * parts[2]), ("n0", n_on), ("n1", n_off), ("n2", n_off), ("n3", n_on)):
+    n_on, n_off, n_all = len(lanes(core, cores[mate])), len(lanes(core, cores[peer])), len(lanes(judge[rank], core))
+    for name, k in (("w1", 2 * n_off), ("c0", 2 * n_off), ("c1", 2 * n_off), ("c2", 2 * n_on), ("n0", n_on), ("n1", n_off),
+                    ("n2", n_off), ("n3", n_on), ("n6", n_on)) + (("n4", n_all), ("n5", n_all)) * OPT["off"]:
         cnt[name] = k
 
     ldq = inc(sy.dma_start(T.qt[:, :], T.qw[:, :]), None, 16)
@@ -338,9 +369,11 @@ def rank_program(g, core, T, topo):
     wait("v", ldq)
     wqd = inc(v.quantize_mx(wcols[0], wcols[1], T.qt[:, :]))
     wait("g", wqd)
-    near_q = [(chooser(mate), T.wq, T.ws, 0, Q, T.wq, T.ws, 2 * Q, "w2")]
-    send_mx([(chooser(other), T.wq, T.ws, 0, Q, T.wq, T.ws, Q, "w1")] + near_q * OPT["fuseq"])
-    send_mx([(cores[peer], T.wq, T.ws, 0, Q, T.wq, T.ws, Q, "w1")])
+    near_q = [(chooser[mate], T.wq, T.ws, 0, Q, T.wq, T.ws, 2 * Q, "w2")]
+    judge_q = [(judge[r], T.wq, T.ws, 0, Q, T.wq, T.ws, Q + Q * place[rank][1], "w1" if OPT["jq"] else "w2")
+               for r in (rank, mate)[:2 - OPT["jq"]] if OPT["off"]]
+    for tos in ([(chooser[other],), (cores[peer],)], [(chooser[other], cores[peer])], [(cores[peer],), (chooser[other],)])[OPT["qm"]]:
+        send_mx([(to, T.wq, T.ws, 0, Q, T.wq, T.ws, Q, "w1") for to in tos])
     wait("v", kz)
     eqd = None
     for b in range(4):
@@ -349,12 +382,13 @@ def rank_program(g, core, T, topo):
     wait("v", ldx)
     xqd = inc(v.quantize_mx(T.xq[:, 0:IT], T.xs[:, 0:IT], T.xr[:, 0:4 * IT]))
     wait("g", xqd)
-    for n, items in enumerate(spread_own(0)):
+    for n, items in enumerate(own_codes(0)):
         send_mx(items)
-        if n == 0 and not OPT["fuseq"]:
+        if n == 0:
             send_mx(near_q)
+            if judge_q and not OPT["late"]:
+                send_mx(judge_q)
     wait("t", xqd, eqd)
-    ybank = [T.y0, T.y1, T.y2, T.y3]
     dm = [inc(pe.matmul_mx(ybank[b][:, 0:IT], T.eq[:, 128 * b:128 * b + 128], T.es[:, 128 * b:128 * b + 128],
                            T.xq[:, 0:IT], T.xs[:, 0:IT], True, True)) for b in range(4)]
     rs = None
@@ -365,24 +399,22 @@ def rank_program(g, core, T, topo):
     wait("v", rs)
     rq = inc(v.quantize_mx(T.xq[:, IT:2 * IT], T.xs[:, IT:2 * IT], T.xr[:, 4 * IT:8 * IT]))
     wait("g", rq)
-    for items in spread_own(1):
+    for items in own_codes(1):
         send_mx(items)
+    if judge_q and OPT["late"]:
+        send_mx(judge_q)
 
-    def landed(q, s, half):
-        wait(q, *[piece_sem(p) for p in lands[core] if p[0] == s and p[1] // IT == half])
-
-    def both(bank, codes, plane, c0, n, out):
+    def both(bank, codes, plane, c0, n, out, q="s"):
         take(bank)
         pe.matmul_mx(bank[:, 0:n], wcols[0], wcols[1], codes[:, c0:c0 + n], plane[:, c0:c0 + n], True, False)
         done = inc(pe.matmul_mx(bank[:, 0:n], wcols[0], wcols[1], codes[:, c0 + n:c0 + 2 * n], plane[:, c0 + n:c0 + 2 * n], False, True))
-        wait("s", done)
-        sem = inc(act.activation(out, bank[:, 0:n], COPY))
+        wait(q, done)
+        sem = inc(act.activation(out, bank[:, 0:n], COPY) if q == "s" else v.tensor_copy(out, bank[:, 0:n]))
         free[bank.name] = [sem]
         return sem
 
-    def spread(b, col, k, done, unit):
-        wait("v", done, kpm)
-        bcd = inc(v.tensor_scalar(T.bc[0:k, 128 * b:128 * b + 128], T.pm[0:k, :], unit, col, MUL, ADD))
+    def spread(b, k, base, s1, s2, op):
+        bcd = inc(v.tensor_scalar(T.bc[0:k, 128 * b:128 * b + 128], base[0:k, :], s1, s2, op, ADD))
         take(T.ob)
         wait("t", bcd)
         return inc(pe.transpose(T.ob[:, 128 * b:128 * b + 128], T.bc[:, 128 * b:128 * b + 128], T.ident[:, :]))
@@ -394,7 +426,7 @@ def rank_program(g, core, T, topo):
         free["ob"] = free.get("ob", []) + [sem]
         return sem
 
-    def pick_from(q, out, win, offs):
+    def pick(q, out, win, offs):
         win = win.indirect(offs)
         return inc(v.tensor_copy(out, win) if q == "v" else act.activation(out, win, COPY))
 
@@ -402,23 +434,15 @@ def rank_program(g, core, T, topo):
         a, vx = 1024 * i, OPT["vx"][i]
         wait("s", ofd, rs)
         wait("v", ofd)
-        cuts = [("s", 512, 1024), ("s", vx, 512), ("v", 0, vx)] if parts[i] == 1 else \
-            [("v", 0, 256), ("s", 256, 512), ("s", 512 + vx // 2, 1024), ("v", 512, 512 + vx // 2)]
-        st["g", i] = []
-        for q, b, e in cuts:
-            if b < e:
-                w = 1024 * (b // 512)
-                st["g", i].append((b, pick_from(q, T.gt[:, a + b:a + e], T.xr[:, w:w + 1024], T.of[:, f + b % 512 // 16:f + (e - 1) % 512 // 16 + 1])))
-            if parts[i] == 2 and e == 512:
-                pack(i, 0, 128)
+        st["g", i] = [pick(q, T.gt[:, a + b:a + e], T.xr[:, 2 * (b // 512 * 512):2 * (b // 512 * 512) + 1024],
+                           T.of[:, f + b % 512 // 16:f + (e - 1) % 512 // 16 + 1])
+                      for q, b, e in (("s", 512, 1024), ("s", vx, 512), ("v", 0, vx)) if b < e]
 
-    def pack(i, b, e):
-        to = hand(rank) if i == 0 and OPT["via"] else cores[(peer, other, mate)[i]]
+    def pack(i):
         c = 256 * i
-        wait("v", *[sem for at, sem in st["g", i] if 4 * b <= at < 4 * e])
-        qz = inc(v.quantize_mx(T.cq[:, c + b:c + e], T.cs[:, c + b:c + e], T.gt[:, 4 * (c + b):4 * (c + e)]))
-        wait("g", qz)
-        send_mx([(to, T.cq, T.cs, c + b, c + e, T.lq, T.ls, c + b, "c%d" % i)])
+        wait("v", *st["g", i])
+        wait("g", inc(v.quantize_mx(T.cq[:, c:c + 256], T.cs[:, c:c + 256], T.gt[:, 4 * c:4 * c + 1024])))
+        send_mx([(chooser[rank] if i == OPT["via"] else cores[(peer, other, mate)[i]], T.cq, T.cs, c, c + 256, T.lq, T.ls, c, "c%d" % i)])
 
     def store(s, n, done):
         wait("y", done)
@@ -427,17 +451,25 @@ def rank_program(g, core, T, topo):
     wait("t", wqd, kid)
     wait("v", ms)
     wait("s", ms)
-    halves = [[over_queries((T.sc0, T.sc1)[h], scores((T.sc0, T.sc1)[h], T.xq, T.xs, 128 * h, 0, Q), 256 * h, Q)] for h in range(2)]
+    halves = [[over_queries((T.sc0, T.sc1)[h], T.xq, T.xs, 128 * h, 0, Q, 256 * h)] for h in range(2)]
+    wait("v", kpm)
+    p16 = inc(v.tensor_scalar(T.p16[:, :], T.pm[:, :], 1.0 / 16.0, None, MUL))
     wait("t", rq)
-    st = {("ab", 0): both(T.y2, T.xq, T.xs, 0, IT, T.ab[:, 0:IT]), "near": [[], []], "row": None}
+    st = {("ab", 0): both(T.y2, T.xq, T.xs, 0, IT, T.ab[:, 0:IT]), "near": [[], []]}
     wait("t", "w1")
     for h in range(2):
-        halves[h].append(over_queries(ybank[h], scores(ybank[h], T.xq, T.xs, 128 * h, Q, Q), 256 * h + Q, Q))
-    first = over_items(0, 0, 16, halves, (T.tr, T.y3))
-    wait("v", spread(0, T.cc[0:16, 0:1], 16, first, T.unit[0:16, :]))
+        halves[h].append(over_queries(ybank[h], T.xq, T.xs, 128 * h, Q, Q, 256 * h + Q))
+    first = over_items(16, halves, (T.tr, T.y3))
+    wait("v", first)
+    wait("v", spread(0, 16, T.pm, T.unit[0:16, :], T.cc[0:16, 0:1], MUL))
     of1 = lists(0, 8, 8)
     of0 = inc(v.tensor_scalar(T.of[:, 32:40], T.ob[:, 0:8], 16.0, None, MUL))
     free["ob"].append(of0)
+    ring = [T.sc0, T.sc1, T.y2, T.y0, T.y1, T.tr, T.y3]
+
+    def bank():
+        ring.append(ring.pop(0))
+        return ring[-1]
 
     def tell():
         wait("g", first)
@@ -445,56 +477,61 @@ def rank_program(g, core, T, topo):
 
     def own():
         wait(OPT["own"], of0, st["ab", 0])
-        store(rank, 1, pick_from(OPT["own"], T.yt[:, 128 * rank:128 * rank + 128], T.ab[:, 0:IT], T.of[:, 32:40]))
+        store(rank, 1, pick(OPT["own"], T.yt[:, 128 * rank:128 * rank + 128], T.ab[:, 0:IT], T.of[:, 32:40]))
 
-    def near(d):
-        banks = ((T.sc0, T.sc1, T.y2, T.y3), (T.y0, T.y1, T.sc0, T.sc1))[d]
-        j0 = place[rank][1]
-        for n, j in enumerate((j0, 1 - j0)):
-            s = whole[d][j]
-            landed("t", s, 0)
-            for h in range(2):
-                bank = banks[2 * n + h]
-                done = scores(bank, T.aq, T["as"], slot(core, s) + 128 * h, 0, Q)
-                st["near"][h].append(over_queries(bank, done, 512 + 512 * h + 128 * (2 * d + j), Q))
+    def near(d, n):
+        j = (place[rank][1] + n) % 2
+        s = whole[d][j]
+        wait("t", *[piece_sem(p) for p in lands[core] if p[0] == s and p[1] < IT])
+        for h in range(2):
+            st["near"][h].append(over_queries(bank(), T.aq, T["as"], slot(core, s) + 128 * h, 0, Q, 512 + 512 * h + 128 * (2 * d + j)))
+
+    def pick_near():
+        assert len(st["near"][0]) == 4
+        st["pick"] = over_items(32, st["near"], (bank(), bank()), 512, 1)
 
     def fwd(i, d):
         for p in lands[core]:
             if (core, p) in onward and p[1] // IT == i and p[0] in whole[d]:
                 forward(p)
 
-    def num():
-        st["num"] = spread(1, T.nx[0:16, 0:1], 16, "n0", 1.0 / 64.0)
+    def num(b):
+        assert b == 1 or ("of", 1) in st
+        wait("v", "n%d" % (3 * b - 3))
+        st["num", b] = spread(b, 8, T.pm, 1.0 / 64.0, T.nx[0:8, 3 * b - 3:3 * b - 2], MUL)
 
-    def num2():
-        wait("v", st["num"])
-        st["of"] = lists(64, 128, 16)
+    def num2(b):
+        wait("v", st["num", b])
+        st["of", b] = lists(48 + 16 * b, 128 * b, 8)
 
-    def ab(d):
-        for j, s in enumerate(whole[d]):
-            landed("t", s, 0)
-            landed("t", s, 1)
-            l = 1 + 2 * d + j
-            st["ab", l] = both(((T.y2, T.y3), (T.y0, T.y1))[d][j], T.aq, T["as"], slot(core, s), IT, T.ab[:, IT * l:IT * l + IT])
+    def ab(d, n):
+        j = (place[rank][1] + n) % 2
+        s, l = whole[d][j], 1 + 2 * d + j
+        wait("t", *[piece_sem(p) for p in lands[core] if p[0] == s])
+        st["ab", l] = both(bank(), T.aq, T["as"], slot(core, s), IT, T.ab[:, IT * l:IT * l + IT], OPT["cp"][2 * d + n])
 
     def fin(i):
         s = (peer, other, mate)[i]
         wait("t", "c%d" % i)
-        store(s, 1, both((T.sc0, T.sc1, T.sc0)[i], T.lq, T.ls, 256 * i, 128, T.yt[:, 128 * s:128 * s + 128]))
-
-    def pick():
-        assert len(st["near"][0]) == 4
-        st["pick"] = over_items(1, 512, 32, st["near"], (T.tr, T.sc1))
+        store(s, 1, both(bank(), T.lq, T.ls, 256 * i, 128, T.yt[:, 128 * s:128 * s + 128], OPT["cp"][4 + i]))
 
     def place1():
-        assert "of" in st
-        st["place"] = spread(2, T.cc[0:32, 4:5], 32, st["pick"], 1.0 / 16.0)
+        assert ("of", 3) in st
+        if not OPT["off"]:
+            wait("v", st["pick"])
+            st["place"] = spread(2, 32, T.pm, 1.0 / 16.0, T.cc[0:32, 4:5], MUL)
+            return
+        wait("v", "n4", "n5", p16)
+        st["place"] = spread(2, 64, T.p16, T.nx[0:64, 4:5], T.nx[0:64, 5:6], ADD)
+
+    def found(l):
+        return 256 + 8 * (4 * (l % 2) + 2 * (l // 2) + place[rank][1] if OPT["off"] else l)
 
     def place2():
         wait("v", st["place"])
         sem = None
         for l in range(4):
-            sem = inc(v.tensor_scalar(T.of[:, 128 + 8 * l:136 + 8 * l], T.ob[:, 256 + 8 * l:264 + 8 * l], 16.0, float(IT * (l % 2)), MUL, ADD), sem)
+            sem = inc(v.tensor_scalar(T.of[:, 128 + 8 * l:136 + 8 * l], T.ob[:, found(l):found(l) + 8], 16.0, float(IT * (l % 2)), MUL, ADD), sem)
         st["ofn"] = sem
 
     def into_row(src):
@@ -507,29 +544,29 @@ def rank_program(g, core, T, topo):
         wait("v", "n1", "n2", "n3")
         wait("v", inc(v.tensor_copy(T.ta[:, 0:96:32], T.nx[0:32, 1:4])))
         wait("v", inc(v.transpose(T.tb[:, :], T.ta[:, :])))
-        st["row"] = into_row({peer: T.tb[0:1, 8:16], other: T.tb[0:1, 32:40], mate: T.tb[0:1, 72:80]})
+        st["row"] = into_row({peer: T.tb[0:1, 8:16], other: T.tb[0:1, 32:40], mate: T.tb[0:1, 64:72]})
 
     def last(d):
-        q = "vs"[d]
+        q = OPT["cp"][7 + d]
         s = whole[d][0]
         wait(q, st["ofn"], st["ab", 1 + 2 * d], st["ab", 2 + 2 * d])
-        store(s, 2, pick_from(q, T.yt[:, 128 * s:128 * s + 256], T.ab[:, IT * (1 + 2 * d):IT * (3 + 2 * d)], T.of[:, 128 + 16 * d:144 + 16 * d]))
+        store(s, 2, pick(q, T.yt[:, 128 * s:128 * s + 256], T.ab[:, IT * (1 + 2 * d):IT * (3 + 2 * d)], T.of[:, 128 + 16 * d:144 + 16 * d]))
 
     def numbers():
         assert st["row"] and "ofn" in st
-        src = {s: T.ob[0:1, 256 + 8 * l:264 + 8 * l] for l, s in enumerate(whole[0] + whole[1])}
+        src = {s: T.ob[0:1, found(l):found(l) + 8] for l, s in enumerate(whole[0] + whole[1])}
         src[rank] = T.ob[0:1, 0:8]
         wait("s", st["row"], into_row(src))
         inc(act.dma_start(T.ch[:, :], T.row[0:1, :]), None, 16)
 
-    steps = {"g1": lambda: gather(0, 0, of1), "g2": lambda: gather(1, 64, st["of"]), "g3": lambda: gather(2, 96, st["of"]),
-             "p1": lambda: pack(0, 128 * (parts[0] - 1), 256), "p2": lambda: pack(1, 128 * (parts[1] - 1), 256),
-             "p3": lambda: pack(2, 128 * (parts[2] - 1), 256), "own": own, "tell": tell,
-             "near0": lambda: near(0), "near1": lambda: near(1), "num": num, "num2": num2,
-             "fx0": lambda: fwd(0, 0), "fx1": lambda: fwd(0, 1), "fR0": lambda: fwd(1, 0), "fR1": lambda: fwd(1, 1),
-             "ab0": lambda: ab(0), "ab1": lambda: ab(1), "fin1": lambda: fin(0), "fin2": lambda: fin(1), "fin3": lambda: fin(2),
-             "pick": pick, "place": place1, "place2": place2, "rows": rows, "last0": lambda: last(0), "last1": lambda: last(1),
-             "ch": numbers}
+    steps = {"g1": lambda: gather(0, 0, of1), "g2": lambda: gather(1, 64, st["of", 1]), "g3": lambda: gather(2, 96, st["of", 3]),
+             "p1": lambda: pack(0), "p2": lambda: pack(1), "p3": lambda: pack(2), "own": own, "tell": tell,
+             "num": lambda: num(1), "num2": lambda: num2(1), "num3": lambda: num(3), "num4": lambda: num2(3),
+             "a00": lambda: ab(0, 0), "a01": lambda: ab(0, 1), "a10": lambda: ab(1, 0), "a11": lambda: ab(1, 1),
+             "fin1": lambda: fin(0), "fin2": lambda: fin(1), "fin3": lambda: fin(2),
+             "n00": lambda: near(0, 0), "n01": lambda: near(0, 1), "n10": lambda: near(1, 0), "n11": lambda: near(1, 1),
+             "pick": pick_near, "fx0": lambda: fwd(0, 0), "fx1": lambda: fwd(0, 1), "fR0": lambda: fwd(1, 0), "fR1": lambda: fwd(1, 1),
+             "place": place1, "place2": place2, "rows": rows, "last0": lambda: last(0), "last1": lambda: last(1), "ch": numbers}
     for name in OPT["order"]:
         steps[name]()
     finish()

from concourse.bass import DstId, RemoteDMATransfer
from concourse.mybir import dt, AluOpType, ActivationFunctionType

NR, Q, IT = 8, 128, 256
LOW = -5.0e29
NCORES = 128
OPT = {
    "route": {("x", 0): "a", ("R", 0): "b", ("x", 1): "ca", ("R", 1): "ca"},
    "split": False, "via": -1, "off": True, "late": 0, "jq": 1, "hr": 0, "qm": 2,
    "lane": {"x0": "A", "R0": "B", "R1": "B"},
    "jo": ["x0", "x1", "n", "R1"], "js": [(0, 0), (0, 1), (1, 0), (1, 1)],
    "vx": [512, 512, 512],
    "own": "s", "cp": list("sssvvsvvs"),
    "order": ["g1", "own", "tell", "p1", "num", "num2", "num3", "g2", "num4", "p2", "g3", "p3", "fin1", "a00", "place", "rows",
              "place2", "a01", "ch", "a10", "last0", "a11", "fin3", "last1", "fin2"],
}

SCRATCH = {
    "qt": ("sbuf", [128, 4 * Q], "bfloat16"),
    "xr": ("sbuf", [128, 8 * IT], "bfloat16"),
    "onb": ("sbuf", [128, 516], "bfloat16"),
    "onf": ("sbuf", [128, 128], "float32"),
    "zt": ("sbuf", [128, 516], "bfloat16"),
    "ident": ("sbuf", [128, 128], "float32"),
    "pm": ("sbuf", [128, 128], "float32"),
    "p16": ("sbuf", [128, 128], "float32"),
    "unit": ("sbuf", [128, 1], "float32"),
    "rst": ("sbuf", [128, 256], "float32"),
    "neg": ("sbuf", [128, 128], "float32"),
    "eq": ("sbuf", [128, 512], "float8_e4m3fn_x4"),
    "es": ("sbuf", [128, 512], "uint8"),
    "wq": ("sbuf", [128, 3 * Q], "float8_e4m3fn_x4"),
    "ws": ("sbuf", [128, 3 * Q], "uint8"),
    "xq": ("sbuf", [128, 2 * IT], "float8_e4m3fn_x4"),
    "xs": ("sbuf", [128, 2 * IT], "uint8"),
    "aq": ("sbuf", [128, 8 * IT], "float8_e4m3fn_x4"),
    "as": ("sbuf", [128, 8 * IT], "uint8"),
    "S": ("sbuf", [128, 2048], "float32"),
    "P": ("sbuf", [128, 512], "float32"),
    "lt": ("sbuf", [128, 32], "float32"),
    "cc": ("sbuf", [128, 8], "float32"),
    "bc": ("sbuf", [128, 512], "float32"),
    "of": ("sbuf", [128, 192], "uint16"),
    "gt": ("sbuf", [128, 3 * 1024], "bfloat16"),
    "cq": ("sbuf", [128, 3 * 256], "float8_e4m3fn_x4"),
    "cs": ("sbuf", [128, 3 * 256], "uint8"),
    "lq": ("sbuf", [128, 3 * 256], "float8_e4m3fn_x4"),
    "ls": ("sbuf", [128, 3 * 256], "uint8"),
    "ab": ("sbuf", [128, 5 * IT], "float32"),
    "yt": ("sbuf", [128, 1024], "float32"),
    "nx": ("sbuf", [128, 8], "float32"),
    "ta": ("sbuf", [32, 96], "float32"),
    "tb": ("sbuf", [32, 96], "float32"),
    "row": ("sbuf", [1, 64], "float32"),
    "sc0": ("psum", [128, 512], "float32"),
    "sc1": ("psum", [128, 512], "float32"),
    "tr": ("psum", [128, 512], "float32"),
    "ob": ("psum", [128, 512], "float32"),
    "y0": ("psum", [128, 512], "float32"),
    "y1": ("psum", [128, 512], "float32"),
    "y2": ("psum", [128, 512], "float32"),
    "y3": ("psum", [128, 512], "float32"),
}
SEMAPHORES = (["lsem", "w1", "w2"] + ["a%d" % i for i in range(16)] + ["c%d" % i for i in range(3)]
              + ["n%d" % i for i in range(7)] + ["u%d" % i for i in range(120)])


def rank_program(g, core, T, topo):
    cores = list(T.cores)
    groups, chips = [], []
    for r in range(len(cores)):
        c = topo.chip(cores[r])
        if c not in chips:
            chips.append(c)
            groups.append([])
        groups[chips.index(c)].append(r)
    ng = len(groups)
    place = {}
    for k in range(ng):
        for j in range(len(groups[k])):
            place[groups[k][j]] = (k, j)
    step = sorted(range(1, ng), key=lambda d: topo.same_plane(chips[0], chips[d]))

    def mate_of(r):
        return groups[place[r][0]][1 - place[r][1]]

    def peer_of(r):
        return groups[(place[r][0] + step[-1]) % ng][place[r][1]]

    def spare(r, other_die, free):
        own = cores[r]
        return [c for c in topo.cores_of(own) if T.rank_of(c) is None and (topo.die(c) != topo.die(own)) == other_die
                and all(topo.may_write(c, t) for t in cores) == free][place[r][1]]

    chooser = [spare(r, True, True) for r in range(len(cores))]
    judge = [spare(r, False, False) for r in range(len(cores))]
    idle = [spare(r, True, False) for r in range(len(cores))]
    relays = [sorted([c for c in range(NCORES) if topo.mates(topo.chip(c), chips[k]) and topo.may_write(c, cores[groups[k][0]])],
                     key=topo.die) for k in range(ng)]

    onward, lands = {}, {}

    def edge(a, piece, b):
        if b not in onward.setdefault((a, piece), []):
            onward[(a, piece)].append(b)
            lands.setdefault(b, []).append(piece)

    for part, c0 in (("x", 0), ("R", IT)):
        for s in range(len(cores)):
            k, j = place[s]
            if part == "x":
                edge(cores[s], (s, 0, IT), chooser[s])
            for d in range(2):
                to = groups[(k + step[d]) % ng]
                way = OPT["route"][(part, d)]
                halves = OPT["split"] and way == "b"
                for h in range(2 if halves else 1):
                    piece = (s, c0 + 128 * h, c0 + 128 * h + 128) if halves else (s, c0, c0 + IT)
                    rl = relays[(k + step[d]) % ng]
                    at = {"c": chooser[s], "b": rl[2 * h + j] if halves else rl[2 * j + d], "a": judge[to[j]], "i": idle[to[j]],
                          "r": cores[to[j]]}
                    stops = [cores[s]] + [at[w] for w in way]
                    for a, b in zip(stops, stops[1:]):
                        edge(a, piece, b)
                    for t in (to[j], to[1 - j])[way[-1] == "r":]:
                        edge(stops[-1], piece, cores[t])

    def slot(c, s):
        r = T.rank_of(c)
        if r is None:
            return 2 * IT * sorted(set(p[0] for p in lands[c])).index(s)
        return 2 * IT * (2 * [(place[r][0] - step[d]) % ng for d in range(2)].index(place[s][0]) + place[s][1])

    queue = {"g": g, "v": g.vector, "s": g.scalar, "t": g.tensor, "y": g.sync}
    cnt, seen, top, pool = {}, {}, {}, [0]

    def inc(ins, name=None, k=1):
        if name is None:
            name = "u%d" % pool[0]
            pool[0] += 1
        ins.then_inc(T.sem[name], k)
        cnt[name] = cnt.get(name, 0) + k
        return name

    def wait(q, *names):
        for name in names:
            v = cnt[name]
            if seen.get((q, name), 0) < v:
                queue[q].wait_ge(T.sem[name], v)
                seen[(q, name)] = v
                top[name] = max(top.get(name, 0), v)

    def finish():
        for name in cnt:
            if top.get(name, 0) < cnt[name]:
                wait("g", name)

    def lanes(a, b, what=None):
        eng = topo.engines(a, b)
        if topo.chip(a) != topo.chip(b):
            w = OPT["lane"].get(what, "8") if a in cores else "8"
            return eng if w == "8" else eng[:len(eng) // 2] if w == "A" else eng[len(eng) // 2:]
        if a in judge or a in idle:
            return eng
        far = [c for c in cores if topo.chip(c) != topo.chip(a) and topo.may_write(a, c)][0]
        return [e for e in eng if e not in topo.engines(a, far)]

    def kind_of(p, b):
        d = [d for d in range(2) if b in relays[(place[p[0]][0] + step[d]) % ng] or topo.chip(b) == chips[(place[p[0]][0] + step[d]) % ng]]
        return "xR"[p[1] // IT] + str(d[0]) if d else None

    def send(items):
        kinds = {}
        for it in items:
            kinds.setdefault(tuple(lanes(core, it[0], *it[5:])), {}).setdefault(it[4], []).append(it)
        moves = []
        for all_eng, kind in kinds.items():
            for n, its in enumerate(kind.values()):
                eng = all_eng[n * len(all_eng) // len(kind):(n + 1) * len(all_eng) // len(kind)]
                moves.append((its, sum(1 << e for e in eng)))
                cnt["lsem"] = cnt.get("lsem", 0) + len(eng)
        if len(items) == 1:
            to, src, dst, sem = items[0][:4]
            rid, pid, _ = topo.addr(to)
            g.remote_dma(out_ap=dst, in_ap=src, remote_sem=T.sem[sem], local_sem=T.sem["lsem"], pid=pid,
                         routing_id=rid, dma_engine_mask=moves[0][1])
            return
        g.remote_dma_fused([RemoteDMATransfer(dst_ids=[DstId(rid=topo.addr(it[0])[0], pnc=topo.addr(it[0])[1]) for it in its],
                                              dma_engine_mask=m, remote_sem=T.sem[its[0][3]], srcs=[its[0][1]],
                                              dsts=[it[2] for it in its]) for its, m in moves], local_sem=T.sem["lsem"])

    def send_mx(items):
        send([(i[0], i[1][:, i[3]:i[4]].bitcast(dt.uint8), i[5][:, i[7]:i[7] + i[4] - i[3]].bitcast(dt.uint8), i[8], (i[3], i[8])) + i[9:]
              for i in items])
        send([(i[0], i[2][:, i[3]:i[4]], i[6][:, i[7]:i[7] + i[4] - i[3]], i[8], (i[3], i[8])) + i[9:] for i in items])

    def piece_sem(piece):
        s, a, e = piece
        return "a%d" % (4 * (2 * (place[s][0] // 2) + place[s][1]) + a // 128)

    def all_pieces(s, half):
        return sorted(set(p for (a, p) in onward if p[0] == s and p[1] // IT == half), key=lambda p: (p[1] - p[2], p[1]))

    for (a, p), tos in onward.items():
        if core in tos:
            share = 2 if a == cores[p[0]] and p[2] - p[1] < IT else 1
            cnt[piece_sem(p)] = cnt.get(piece_sem(p), 0) + 2 * len(lanes(a, core, kind_of(p, core) if a == cores[p[0]] else None)) // share

    def own_codes(half):
        calls = []
        for p in all_pieces(rank, half):
            for t in onward.get((core, p), []):
                it = (t, T.xq, T.xs, p[1], p[2], T.aq, T["as"], slot(t, p[0]) + p[1], piece_sem(p), kind_of(p, t))
                mine = set(lanes(core, t, it[9]))
                fit = [c for c in calls if c[0][4] - c[0][3] == p[2] - p[1]
                       and all(mine.isdisjoint(lanes(core, o[0], o[9])) or (o[9] == it[9] and o[3] != it[3]) for o in c)]
                if fit:
                    fit[0].append(it)
                else:
                    calls.append([it])
        return calls

    def forward(p):
        wait("g", piece_sem(p))
        a = slot(core, p[0])
        for t in onward[(core, p)]:
            send_mx([(t, T.aq, T["as"], a + p[1], a + p[2], T.aq, T["as"], slot(t, p[0]) + p[1], piece_sem(p))])

    v, pe, act, sy = g.vector, g.tensor, g.scalar, g.sync
    COPY, SIGN = ActivationFunctionType.Copy, ActivationFunctionType.Sign
    ADD, MAX, MUL = AluOpType.add, AluOpType.max, AluOpType.mult
    free = {}

    def take(bank):
        wait("t", *free.get(bank.name, []))
        free[bank.name] = []

    def constants():
        one = inc(v.memset(T.onf[:, :], 1.0))
        z = inc(v.memset(T.rst[:, :], 0.0))
        ms = inc(v.memset(T.neg[:, :], LOW))
        inc(v.memset(T.cc[:, :], 0.0), ms)
        wait("v", z)
        inc(v.memset(T.rst[:, 0:256:16], LOW), ms)
        wait("g", one)
        kid = inc(g.affine_select(T.ident[:, :], T.onf[:, :], [[-1, 128]], AluOpType.is_equal, 0.0, 0, 1))
        return ms, kid

    def over_queries(bank, codes, plane, c0, w0, n, at):
        take(bank)
        wait("v", inc(pe.matmul_mx(bank[:, 0:n], codes[:, c0:c0 + 128], plane[:, c0:c0 + 128], T.wq[:, w0:w0 + n], T.ws[:, w0:w0 + n], True, True)))
        sem = inc(v.tensor_tensor_scan(T.S[:, at:at + n], T.rst[:, 0:n], bank[:, 0:n], 0.0, ADD, MAX))
        free[bank.name] = [sem]
        return sem

    def over_items(k, halves, banks, at=0, b=0):
        run, p = LOW, 256 * b
        for h in range(2):
            take(banks[h])
            wait("t", *halves[h])
            done = inc(pe.transpose(banks[h][0:k, 0:128], T.S[:, at + 16 * k * h + 15:at + 16 * k * (h + 1):16], T.ident[:, :]))
            wait("v", done, *free[banks[0].name])
            sem = inc(v.tensor_tensor_scan(T.P[0:k, p + 128 * h:p + 128 * h + 128], banks[h][0:k, 0:128], T.neg[0:k, :], run, MAX, MAX))
            free[banks[h].name] = [sem]
            run = T.P[0:k, p + 127:p + 128]
        wait("s", sem)
        return inc(act.activation(T.lt[0:k, 16 * b:16 * b + 16], T.P[0:k, p + 15:p + 256:16], SIGN, bias=T.P[0:k, p + 255:p + 256],
                                  scale=-1.0, accum_out=T.cc[0:k, 4 * b:4 * b + 1]))

    rank = T.rank_of(core)
    ybank = [T.y0, T.y1, T.y2, T.y3]
    if rank is None:
        if core not in lands:
            return
        col = T.cc[:, 0:1]
        jobs = sorted([p for p in lands[core] if (core, p) in onward], key=lambda p: p[1])
        judging = core in judge and OPT["off"]
        if core in chooser or judging:
            ms, kid = constants()
            wait("t", kid)
            wait("v", ms)
            wait("s", ms)
        tell = []
        if core in chooser:
            s = chooser.index(core)
            far = mate_of(peer_of(s))
            cnt["w1"] = 2 * len(lanes(cores[far], core))
            cnt["w2"] = 2 * len(lanes(cores[s], core))
            wait("t", piece_sem((s, 0, IT)), "w1")
            one = over_items(8, [[over_queries(ybank[h], T.aq, T["as"], 128 * h, Q, Q, 128 * h)] for h in range(2)], (T.tr, T.ob))
            wait("t", "w2")
            two = over_items(8, [[over_queries(ybank[2 + h], T.aq, T["as"], 128 * h, 2 * Q, Q, 256 + 128 * h)] for h in range(2)],
                             (T.tr, T.ob), 256, 1)
            tell = [(one, [(cores[s], col, T.nx[:, 0:1], "n0", 0), (cores[far], col, T.nx[:, 2:3], "n2", 1)]),
                    (two, [(cores[s], T.cc[:, 4:5], T.nx[:, 6:7], "n6", 0)]),
                    (two, [(cores[mate_of(s)], T.cc[:, 4:5], T.nx[:, 3:4], "n3", 0)])]
        if judging:
            k, j = place[judge.index(core)]
            wait("v", inc(v.memset(T.S[:, 15:2048:16], 0.0)))
            if OPT["jq"]:
                twin = judge[groups[k][1 - j]]
                cnt["w1"], cnt["w2"] = 2 * len(lanes(cores[groups[k][j]], core)), 2 * len(lanes(twin, core))
                wait("g", "w1")
                send_mx([(twin, T.wq, T.ws, Q + Q * j, 2 * Q + Q * j, T.wq, T.ws, Q + Q * j, "w2")])
                wait("t", "w1")
            else:
                cnt["w2"] = sum(2 * len(lanes(cores[r], core)) for r in groups[k])
                wait("t", "w2")
            halves = [[], []]
            six = ybank + [T.sc0, T.sc1]
            for n, (d, far) in enumerate(OPT["js"]):
                s = groups[(k - step[d]) % ng][j]
                i = (j + far) % 2
                wait("t", piece_sem((s, 0, IT)), *["w2"] * far)
                for h in range(2):
                    halves[h].append(over_queries(six[(2 * n + h) % 6], T.aq, T["as"], slot(core, s) + 128 * h, Q + Q * i, Q,
                                                  1024 * h + 256 * (2 * j + d) + 128 * i))
            chosen = over_items(64, halves, (T.tr, T.ob))
            for what in OPT["jo"]:
                if what == "n":
                    wait("g", chosen)
                    send([(cores[r], col, T.nx[:, 4 + j:5 + j], "n%d" % (4 + j), 0) for r in groups[k]])
                for p in jobs:
                    if what == "xR"[p[1] // IT] + str([(k - step[d]) % ng for d in range(2)].index(place[p[0]][0])):
                        forward(p)
            jobs = []
        for p in jobs:
            if p[1] < IT:
                forward(p)
        for n, (done, items) in enumerate(tell):
            wait("g", done)
            send(items)
            for p in jobs:
                if p[1] >= IT and n == OPT["hr"]:
                    forward(p)
        for p in jobs:
            if p[1] >= IT and not tell:
                forward(p)
        if core in chooser and OPT["via"] >= 0:
            i, s = OPT["via"], chooser.index(core)
            cnt["c%d" % i] = 2 * len(lanes(cores[s], core))
            wait("g", "c%d" % i)
            send_mx([(cores[(peer_of(s), mate_of(peer_of(s)))[i]], T.lq, T.ls, 256 * i, 256 * i + 256, T.lq, T.ls, 256 * i, "c%d" % i)])
        finish()
        return

    mate, peer = mate_of(rank), peer_of(rank)
    other = mate_of(peer)
    whole = [groups[(place[rank][0] - step[d]) % ng] for d in range(2)]
    wcols = T.wq[:, 0:Q], T.ws[:, 0:Q]
    n_on, n_off, n_all = len(lanes(core, cores[mate])), len(lanes(core, cores[peer])), len(lanes(judge[rank], core))
    for name, k in (("w1", 2 * n_off), ("c0", 2 * n_off), ("c1", 2 * n_off), ("c2", 2 * n_on), ("n0", n_on), ("n1", n_off),
                    ("n2", n_off), ("n3", n_on), ("n6", n_on)) + (("n4", n_all), ("n5", n_all)) * OPT["off"]:
        cnt[name] = k

    ldq = inc(sy.dma_start(T.qt[:, :], T.qw[:, :]), None, 16)
    ldx = inc(act.dma_start(T.xr[:, 0:4 * IT], T.x[:, :]), None, 16)
    kone = inc(v.memset(T.onb[:, :], 1.0))
    wait("g", kone)
    kz = inc(g.affine_select(T.zt[:, :], T.onb[:, :], [[-1, 516]], AluOpType.is_equal, 0.0, 3, 4))
    ms, kid = constants()
    kpm = inc(g.iota(T.pm[:, :], [[0, 8], [1, 16]], 0, 0, allow_small_or_imprecise_dtypes=True))
    inc(v.memset(T.bc[:, :], 0.0), ms)
    inc(v.memset(T.ta[:, :], 0.0), ms)
    un = inc(v.memset(T.unit[:, :], 1.0 / 64.0))
    wait("v", un)
    inc(v.memset(T.unit[0:8, :], 1.0 / 16.0), ms)

    wait("v", ldq)
    wqd = inc(v.quantize_mx(wcols[0], wcols[1], T.qt[:, :]))
    wait("g", wqd)
    near_q = [(chooser[mate], T.wq, T.ws, 0, Q, T.wq, T.ws, 2 * Q, "w2")]
    judge_q = [(judge[r], T.wq, T.ws, 0, Q, T.wq, T.ws, Q + Q * place[rank][1], "w1" if OPT["jq"] else "w2")
               for r in (rank, mate)[:2 - OPT["jq"]] if OPT["off"]]
    for tos in ([(chooser[other],), (cores[peer],)], [(chooser[other], cores[peer])], [(cores[peer],), (chooser[other],)])[OPT["qm"]]:
        send_mx([(to, T.wq, T.ws, 0, Q, T.wq, T.ws, Q, "w1") for to in tos])
    wait("v", kz)
    eqd = None
    for b in range(4):
        eqd = inc(v.quantize_mx(T.eq[:, 128 * b:128 * b + 128], T.es[:, 128 * b:128 * b + 128], T.zt[:, 3 - b:3 - b + 512]), eqd)

    wait("v", ldx)
    xqd = inc(v.quantize_mx(T.xq[:, 0:IT], T.xs[:, 0:IT], T.xr[:, 0:4 * IT]))
    wait("g", xqd)
    for n, items in enumerate(own_codes(0)):
        send_mx(items)
        if n == 0:
            send_mx(near_q)
            if judge_q and not OPT["late"]:
                send_mx(judge_q)
    wait("t", xqd, eqd)
    dm = [inc(pe.matmul_mx(ybank[b][:, 0:IT], T.eq[:, 128 * b:128 * b + 128], T.es[:, 128 * b:128 * b + 128],
                           T.xq[:, 0:IT], T.xs[:, 0:IT], True, True)) for b in range(4)]
    rs = None
    for b in range(4):
        wait("v", dm[b])
        rs = inc(v.tensor_tensor(T.xr[:, 4 * IT + b:8 * IT:4], T.xr[:, b:4 * IT:4], ybank[b][:, 0:IT], AluOpType.subtract), rs)
        free[ybank[b].name] = [rs]
    wait("v", rs)
    rq = inc(v.quantize_mx(T.xq[:, IT:2 * IT], T.xs[:, IT:2 * IT], T.xr[:, 4 * IT:8 * IT]))
    wait("g", rq)
    for items in own_codes(1):
        send_mx(items)
    if judge_q and OPT["late"]:
        send_mx(judge_q)

    def both(bank, codes, plane, c0, n, out, q="s"):
        take(bank)
        pe.matmul_mx(bank[:, 0:n], wcols[0], wcols[1], codes[:, c0:c0 + n], plane[:, c0:c0 + n], True, False)
        done = inc(pe.matmul_mx(bank[:, 0:n], wcols[0], wcols[1], codes[:, c0 + n:c0 + 2 * n], plane[:, c0 + n:c0 + 2 * n], False, True))
        wait(q, done)
        sem = inc(act.activation(out, bank[:, 0:n], COPY) if q == "s" else v.tensor_copy(out, bank[:, 0:n]))
        free[bank.name] = [sem]
        return sem

    def spread(b, k, base, s1, s2, op):
        bcd = inc(v.tensor_scalar(T.bc[0:k, 128 * b:128 * b + 128], base[0:k, :], s1, s2, op, ADD))
        take(T.ob)
        wait("t", bcd)
        return inc(pe.transpose(T.ob[:, 128 * b:128 * b + 128], T.bc[:, 128 * b:128 * b + 128], T.ident[:, :]))

    def lists(f, c0, k):
        sem = None
        for u in range(4):
            sem = inc(v.tensor_scalar(T.of[:, f + u:f + 4 * k:4], T.ob[:, c0:c0 + k], 64.0, float(16 * u), MUL, ADD), sem)
        free["ob"] = free.get("ob", []) + [sem]
        return sem

    def pick(q, out, win, offs):
        win = win.indirect(offs)
        return inc(v.tensor_copy(out, win) if q == "v" else act.activation(out, win, COPY))

    def gather(i, f, ofd):
        a, vx = 1024 * i, OPT["vx"][i]
        wait("s", ofd, rs)
        wait("v", ofd)
        st["g", i] = [pick(q, T.gt[:, a + b:a + e], T.xr[:, 2 * (b // 512 * 512):2 * (b // 512 * 512) + 1024],
                           T.of[:, f + b % 512 // 16:f + (e - 1) % 512 // 16 + 1])
                      for q, b, e in (("s", 512, 1024), ("s", vx, 512), ("v", 0, vx)) if b < e]

    def pack(i):
        c = 256 * i
        wait("v", *st["g", i])
        wait("g", inc(v.quantize_mx(T.cq[:, c:c + 256], T.cs[:, c:c + 256], T.gt[:, 4 * c:4 * c + 1024])))
        send_mx([(chooser[rank] if i == OPT["via"] else cores[(peer, other, mate)[i]], T.cq, T.cs, c, c + 256, T.lq, T.ls, c, "c%d" % i)])

    def store(s, n, done):
        wait("y", done)
        inc(sy.dma_start(T.y[:, 128 * s:128 * (s + n)], T.yt[:, 128 * s:128 * (s + n)]), None, 16)

    wait("t", wqd, kid)
    wait("v", ms)
    wait("s", ms)
    halves = [[over_queries((T.sc0, T.sc1)[h], T.xq, T.xs, 128 * h, 0, Q, 256 * h)] for h in range(2)]
    wait("v", kpm)
    p16 = inc(v.tensor_scalar(T.p16[:, :], T.pm[:, :], 1.0 / 16.0, None, MUL))
    wait("t", rq)
    st = {("ab", 0): both(T.y2, T.xq, T.xs, 0, IT, T.ab[:, 0:IT]), "near": [[], []]}
    wait("t", "w1")
    for h in range(2):
        halves[h].append(over_queries(ybank[h], T.xq, T.xs, 128 * h, Q, Q, 256 * h + Q))
    first = over_items(16, halves, (T.tr, T.y3))
    wait("v", first)
    wait("v", spread(0, 16, T.pm, T.unit[0:16, :], T.cc[0:16, 0:1], MUL))
    of1 = lists(0, 8, 8)
    of0 = inc(v.tensor_scalar(T.of[:, 32:40], T.ob[:, 0:8], 16.0, None, MUL))
    free["ob"].append(of0)
    ring = [T.sc0, T.sc1, T.y2, T.y0, T.y1, T.tr, T.y3]

    def bank():
        ring.append(ring.pop(0))
        return ring[-1]

    def tell():
        wait("g", first)
        send([(cores[peer], T.cc[:, 0:1], T.nx[:, 1:2], "n1", 0)])

    def own():
        wait(OPT["own"], of0, st["ab", 0])
        store(rank, 1, pick(OPT["own"], T.yt[:, 128 * rank:128 * rank + 128], T.ab[:, 0:IT], T.of[:, 32:40]))

    def near(d, n):
        j = (place[rank][1] + n) % 2
        s = whole[d][j]
        wait("t", *[piece_sem(p) for p in lands[core] if p[0] == s and p[1] < IT])
        for h in range(2):
            st["near"][h].append(over_queries(bank(), T.aq, T["as"], slot(core, s) + 128 * h, 0, Q, 512 + 512 * h + 128 * (2 * d + j)))

    def pick_near():
        assert len(st["near"][0]) == 4
        st["pick"] = over_items(32, st["near"], (bank(), bank()), 512, 1)

    def fwd(i, d):
        for p in lands[core]:
            if (core, p) in onward and p[1] // IT == i and p[0] in whole[d]:
                forward(p)

    def num(b):
        assert b == 1 or ("of", 1) in st
        wait("v", "n%d" % (3 * b - 3))
        st["num", b] = spread(b, 8, T.pm, 1.0 / 64.0, T.nx[0:8, 3 * b - 3:3 * b - 2], MUL)

    def num2(b):
        wait("v", st["num", b])
        st["of", b] = lists(48 + 16 * b, 128 * b, 8)

    def ab(d, n):
        j = (place[rank][1] + n) % 2
        s, l = whole[d][j], 1 + 2 * d + j
        wait("t", *[piece_sem(p) for p in lands[core] if p[0] == s])
        st["ab", l] = both(bank(), T.aq, T["as"], slot(core, s), IT, T.ab[:, IT * l:IT * l + IT], OPT["cp"][2 * d + n])

    def fin(i):
        s = (peer, other, mate)[i]
        wait("t", "c%d" % i)
        store(s, 1, both(bank(), T.lq, T.ls, 256 * i, 128, T.yt[:, 128 * s:128 * s + 128], OPT["cp"][4 + i]))

    def place1():
        assert ("of", 3) in st
        if not OPT["off"]:
            wait("v", st["pick"])
            st["place"] = spread(2, 32, T.pm, 1.0 / 16.0, T.cc[0:32, 4:5], MUL)
            return
        wait("v", "n4", "n5", p16)
        st["place"] = spread(2, 64, T.p16, T.nx[0:64, 4:5], T.nx[0:64, 5:6], ADD)

    def found(l):
        return 256 + 8 * (4 * (l % 2) + 2 * (l // 2) + place[rank][1] if OPT["off"] else l)

    def place2():
        wait("v", st["place"])
        sem = None
        for l in range(4):
            sem = inc(v.tensor_scalar(T.of[:, 128 + 8 * l:136 + 8 * l], T.ob[:, found(l):found(l) + 8], 16.0, float(IT * (l % 2)), MUL, ADD), sem)
        st["ofn"] = sem

    def into_row(src):
        sem = None
        for s in src:
            sem = inc(v.tensor_copy(T.row[0:1, s:64:8], src[s]), sem)
        return sem

    def rows():
        wait("v", "n1", "n2", "n3")
        wait("v", inc(v.tensor_copy(T.ta[:, 0:96:32], T.nx[0:32, 1:4])))
        wait("v", inc(v.transpose(T.tb[:, :], T.ta[:, :])))
        st["row"] = into_row({peer: T.tb[0:1, 8:16], other: T.tb[0:1, 32:40], mate: T.tb[0:1, 64:72]})

    def last(d):
        q = OPT["cp"][7 + d]
        s = whole[d][0]
        wait(q, st["ofn"], st["ab", 1 + 2 * d], st["ab", 2 + 2 * d])
        store(s, 2, pick(q, T.yt[:, 128 * s:128 * s + 256], T.ab[:, IT * (1 + 2 * d):IT * (3 + 2 * d)], T.of[:, 128 + 16 * d:144 + 16 * d]))

    def numbers():
        assert st["row"] and "ofn" in st
        src = {s: T.ob[0:1, found(l):found(l) + 8] for l, s in enumerate(whole[0] + whole[1])}
        src[rank] = T.ob[0:1, 0:8]
        wait("s", st["row"], into_row(src))
        inc(act.dma_start(T.ch[:, :], T.row[0:1, :]), None, 16)

    steps = {"g1": lambda: gather(0, 0, of1), "g2": lambda: gather(1, 64, st["of", 1]), "g3": lambda: gather(2, 96, st["of", 3]),
             "p1": lambda: pack(0), "p2": lambda: pack(1), "p3": lambda: pack(2), "own": own, "tell": tell,
             "num": lambda: num(1), "num2": lambda: num2(1), "num3": lambda: num(3), "num4": lambda: num2(3),
             "a00": lambda: ab(0, 0), "a01": lambda: ab(0, 1), "a10": lambda: ab(1, 0), "a11": lambda: ab(1, 1),
             "fin1": lambda: fin(0), "fin2": lambda: fin(1), "fin3": lambda: fin(2),
             "n00": lambda: near(0, 0), "n01": lambda: near(0, 1), "n10": lambda: near(1, 0), "n11": lambda: near(1, 1),
             "pick": pick_near, "fx0": lambda: fwd(0, 0), "fx1": lambda: fwd(0, 1), "fR0": lambda: fwd(1, 0), "fR1": lambda: fwd(1, 1),
             "place": place1, "place2": place2, "rows": rows, "last0": lambda: last(0), "last1": lambda: last(1), "ch": numbers}
    for name in OPT["order"]:
        steps[name]()
    finish()
